import numpy as np
import ml_dtypes


def mxq(x, axis, fmt="e4m3"):
    dtype, down = {"e4m3": (ml_dtypes.float8_e4m3fn, 7), "e5m2": (ml_dtypes.float8_e5m2, 14)}[fmt]
    v = np.moveaxis(np.asarray(x, np.float32).astype(ml_dtypes.bfloat16).astype(np.float64), axis, -1)
    blocks = v.reshape(v.shape[:-1] + (-1, 32))
    amax = np.abs(blocks).max(-1, keepdims=True)
    byte = np.maximum(np.where(amax > 0, np.frexp(amax)[1] - 1 + 127, 0) - down, 1)
    scale = np.exp2(byte - 127.0)
    codes = (blocks / scale).astype(np.float32).astype(dtype).astype(np.float64)
    return np.moveaxis((codes * scale).reshape(v.shape), -1, axis)


WIDE = False


def mx_kscale(k):
    if not WIDE:
        return np.ones(k)
    levels = np.array([10, -10, 5, -5, 0])
    if k % 512:
        return np.exp2(np.random.permutation(np.resize(levels, k // 32))).repeat(32)
    a = np.empty((k // 512, 16))
    for p in range(k // 512):
        a[p, :8] = np.random.permutation(np.resize(levels, 8))
        for g in range(8):
            far = levels[np.abs(levels - a[p, g]) >= 10]
            a[p, g + 8] = far[np.random.randint(len(far))]
    return np.exp2(a.ravel()).repeat(32)


BF16 = ml_dtypes.bfloat16


def bf(x):
    return np.asarray(x, np.float32).astype(BF16)


def f64(x):
    return np.asarray(x).astype(np.float64)


T, HEADS, D, V = 512, 4, 1024, 1024


def draw0():
    s = mx_kscale(D)
    u = mx_kscale(HEADS * T)
    x = np.random.standard_normal((T, D)) * s
    r = np.random.standard_normal((T, D))
    w = np.random.standard_normal((D, HEADS * D)) / np.sqrt(D) / s[:, None]
    c = np.random.uniform(0.5, 1.5, HEADS * T) * u
    g = np.random.standard_normal((HEADS * T, V)) / np.sqrt(HEADS * T) / u[:, None]
    return {"x": bf(x),
            "r": bf(r),
            "w": bf(w),
            "c": bf(c.reshape(HEADS, T)),
            "g": bf(g)}


def core(x, r, w, c, g):
    z = mxq(f64(x), 1, "e4m3") @ mxq(f64(w), 0, "e4m3")
    z = z.reshape(T, HEADS, D).transpose(1, 0, 2)
    h = (z / (1.0 + np.exp(-z)) + f64(r)) * f64(c).reshape(HEADS, T, 1)
    h = h.reshape(HEADS * T, D)
    du = mxq(h, 0, "e4m3").T @ mxq(f64(g), 0, "e4m3")
    return du


def e4m3fn_bytes(y):
    return np.clip(np.asarray(y, np.float64), -448.0, 448.0).astype(np.float32).astype(ml_dtypes.float8_e4m3fn).view(np.uint8)


def e4m3fn_values(b):
    return np.asarray(b, np.uint8).view(ml_dtypes.float8_e4m3fn).astype(np.float64)


def setup_inputs():
    d = draw0()
    x0 = np.asarray(d['w']).astype(np.float64)
    s = (np.max(np.abs(x0), axis=(1,), keepdims=True) / 448.0).astype(np.float32)
    out = {}
    for k, v in d.items():
        if k == 'w':
            out['w_bytes'] = e4m3fn_bytes(x0 / s.astype(np.float64))
            out['w_scale'] = s
        else:
            out[k] = v
    return out


def reference(x, r, w_bytes, w_scale, c, g):
    return core(x, r, e4m3fn_values(w_bytes) * w_scale.astype(np.float64), c, g)

@@ -1,0 +1,352 @@
+from contextlib import ExitStack
+
+import concourse.mybir as mybir
+from concourse.masks import make_identity
+
+T, HEADS, D, V = 512, 4, 1024, 1024
+FLOPS = 2 * T * D * HEADS * D + 2 * D * HEADS * T * V
+
+F32 = mybir.dt.float32
+BF16 = mybir.dt.bfloat16
+U32 = mybir.dt.uint32
+U8 = mybir.dt.uint8
+E4M3 = mybir.dt.float8_e4m3fn
+FP8X4 = mybir.dt.float8_e4m3fn_x4
+ACT = mybir.ActivationFunctionType
+ALU = mybir.AluOpType
+ENG = mybir.EngineType
+
+P = 128
+PACK = 4
+PASSES = D // 512
+W = 512
+UNITS = 8
+
+V_WIDEN = {0: 4, 1: 2, 4: 1}
+S_INTER_W = set()
+S_INTER_G = {(1, 0), (1, 1), (2, 0), (2, 1), (3, 0)}
+S_INTER_H = {5, 10}
+V_EMIT = {(4, 1), (7, 0)}
+ITEMS = [(j, 0, 512) for j in range(HEADS)] + [(j, lo, 256) for lo in (512, 768) for j in range(HEADS)]
+
+
+def tile_medusa_unembedding_grad_s7_kernel(tc, x, r, w_bytes, w_scale, c, g, out):
+    nc = tc.nc
+    with ExitStack() as ctx:
+        ctx.enter_context(tc.manual_schedule(engines={ENG.DVE, ENG.Activation, ENG.Pool, ENG.SP}))
+        keep = ctx.enter_context(tc.tile_pool(name="keep", bufs=1))
+        pool = ctx.enter_context(tc.tile_pool(name="pool", bufs=2))
+        psum = ctx.enter_context(tc.psum_pool(name="psum", bufs=3))
+
+        ws = keep.tile([P, PASSES, PACK], F32, name="ws")
+        c16 = keep.tile([P, HEADS, PACK], BF16, name="c16")
+        c32 = keep.tile([P, HEADS, PACK], F32, name="c32")
+        ident = keep.tile([P, P], F32, name="ident")
+        ident16 = keep.tile([P, P], BF16, name="ident16")
+        diag = keep.tile([P, HEADS * PACK, P], BF16, name="diag")
+        warm = keep.tile([P, 1], F32, name="warm")
+        x_raw = keep.tile([P, PACK, D], BF16, name="x_raw", align_bytes=64)
+        x_grp = keep.tile([P, PASSES, PACK, P, PACK], BF16, name="x_grp", align_bytes=64)
+        x_codes = keep.tile([P, PASSES, T], U32, name="x_codes", align_bytes=64)
+        x_scales = keep.tile([P, PASSES, T], U8, name="x_scales", align_bytes=64)
+        r_sb = keep.tile([P, PACK, D], BF16, name="r_sb")
+        g_codes = keep.tile([P, HEADS, V], U32, name="g_codes", align_bytes=64)
+        g_scales = keep.tile([P, HEADS, V], U8, name="g_scales", align_bytes=64)
+        h_codes = keep.tile([P, HEADS, D], U32, name="h_codes", align_bytes=64)
+        h_scales = keep.tile([P, HEADS, D], U8, name="h_scales", align_bytes=64)
+
+        w_view = w_bytes.rearrange("(g p t) (j h n) -> g j h p t n", p=P, t=PACK, j=HEADS, h=2)
+        g_view = g.rearrange("(j p t) v -> j p t v", p=P, t=PACK)
+
+        w8 = {}
+        wide = {}
+        w_grp = {}
+        w_codes = {}
+        w_scales = {}
+        g_raw = {}
+        g_grp = {}
+        sil = {}
+        h_raw = {}
+        h_grp = {}
+        z_ps = {}
+        rc_ps = {}
+        acc = {}
+
+        def load_w(u):
+            for gg in range(PASSES):
+                t = pool.tile([P, PACK, W], U8, name="w8", bufs=16)
+                nc.sync.dma_start(out=t[:], in_=w_view[gg, u % 4, u // 4])
+                w8[u, gg] = t
+
+        def load_g(j):
+            t = pool.tile([P, PACK, V], BF16, name="g_raw", bufs=3)
+            nc.sync.dma_start(out=t[:], in_=g_view[j])
+            g_raw[j] = t
+
+        def widen(u, i):
+            gg, t = i // PACK, i % PACK
+            if t == 0:
+                wide[u, gg] = pool.tile([P, PACK, W], BF16, name="wide", bufs=4, align_bytes=64)
+            src = w8[u, gg][:, t, :].bitcast(E4M3)
+            dst = wide[u, gg][:, t, :]
+            if i % 2 == 1 and i // 2 < V_WIDEN.get(u, 0):
+                nc.vector.tensor_scalar(out=dst, in0=src, scalar1=ws[:, gg, t : t + 1], scalar2=None, op0=ALU.mult)
+            else:
+                nc.scalar.activation(out=dst, in_=src, func=ACT.Copy, scale=ws[:, gg, t : t + 1])
+
+        def interleave(engine, dst, src):
+            d4 = dst.rearrange("p (c i) t -> p c t i", i=4)
+            s4 = src.rearrange("p t (c i) -> p c t i", i=4)
+            if engine == "v":
+                nc.vector.tensor_copy(out=d4, in_=s4)
+            else:
+                nc.scalar.copy(out=d4, in_=s4)
+
+        def inter_w(u, gg):
+            engine = "s" if (u, gg) in S_INTER_W else "v"
+            t = pool.tile([P, W, PACK], BF16, name="w_grp", bufs=3, align_bytes=64)
+            interleave(engine, t[:], wide[u, gg][:])
+            w_grp[u, gg] = t
+
+        def quantize(codes, scales, src):
+            nc.vector.quantize_mx(out=codes.bitcast(FP8X4), scales=scales, in_=src)
+
+        def quant_w(u, gg):
+            tc_ = pool.tile([P, W], U32, name="w_codes", bufs=10, align_bytes=64)
+            ts_ = pool.tile([P, W], U8, name="w_scales", bufs=10, align_bytes=64)
+            quantize(tc_[:], ts_[:], w_grp[u, gg][:].rearrange("p n t -> p (n t)"))
+            w_codes[u, gg] = tc_
+            w_scales[u, gg] = ts_
+
+        def inter_g(j, half):
+            engine = "s" if (j, half) in S_INTER_G else "v"
+            t = pool.tile([P, W, PACK], BF16, name="g_grp", bufs=3, align_bytes=64)
+            interleave(engine, t[:], g_raw[j][:, :, half * W : (half + 1) * W])
+            g_grp[j, half] = t
+
+        def quant_g(j, half):
+            cols = slice(half * W, (half + 1) * W)
+            quantize(g_codes[:, j, cols], g_scales[:, j, cols], g_grp[j, half][:].rearrange("p n t -> p (n t)"))
+
+        def x_transpose(gg, pair, tag):
+            bank = psum.tile([P, 2, 2, P], F32, name="x_ps", tag=tag, bufs=3)
+            words = x_raw[:].bitcast(F32)
+            for b in range(2):
+                for e in range(2):
+                    lo = 256 * gg
+                    nc.tensor.transpose(bank[:, b, e, :], words[:, 2 * pair + b, lo + e : lo + 256 : 2], ident[:])
+            return bank
+
+        def x_copy(gg, pair, bank, engine):
+            dst = x_grp[:, gg, 2 * pair : 2 * pair + 2].rearrange("p b m k -> p b (m k)").bitcast(F32)
+            dst = dst.rearrange("p b (m e) -> p b m e", e=2)
+            src = bank[:].rearrange("p b e m -> p b m e")
+            if engine == "v":
+                nc.vector.tensor_copy(out=dst, in_=src)
+            else:
+                nc.scalar.copy(out=dst, in_=src)
+
+        def quant_x(gg):
+            quantize(x_codes[:, gg, :], x_scales[:, gg, :], x_grp[:, gg].rearrange("p b m k -> p (b m k)"))
+
+        def slots_of(k, i):
+            width = ITEMS[k][2]
+            per = W // width
+            return [i * per + b for b in range(per)]
+
+        def chunks(k):
+            return ITEMS[k][2] * PACK // W
+
+        def zmm(k, i):
+            j, lo, width = ITEMS[k]
+            u, off = (lo // W) * 4 + j, lo % W
+            z = psum.tile([P, W], F32, name="z_ps", tag="z", bufs=3)
+            for b, t in enumerate(slots_of(k, i)):
+                rows = slice(t * P, (t + 1) * P)
+                for gg in range(PASSES):
+                    nc.tensor.matmul_mx(
+                        out=z[:, b * width : (b + 1) * width],
+                        lhsT=x_codes[:, gg, rows].bitcast(FP8X4),
+                        lhsT_scale=x_scales[:, gg, rows],
+                        rhs=w_codes[u, gg][:, off : off + width].bitcast(FP8X4),
+                        rhs_scale=w_scales[u, gg][:, off : off + width],
+                        start=(gg == 0),
+                        stop=(gg == PASSES - 1),
+                    )
+            z_ps[k, i] = z
+
+        def rcmm(k, i):
+            j, lo, width = ITEMS[k]
+            rc = psum.tile([P, W], F32, name="rc_ps", tag="rc", bufs=2)
+            for b, t in enumerate(slots_of(k, i)):
+                nc.tensor.matmul(
+                    out=rc[:, b * width : (b + 1) * width],
+                    lhsT=diag[:, j * PACK + t, :],
+                    rhs=r_sb[:, t, lo : lo + width],
+                    start=True,
+                    stop=True,
+                )
+            rc_ps[k, i] = rc
+
+        def silu(k, i):
+            j, lo, width = ITEMS[k]
+            slots = slots_of(k, i)
+            if i == 0:
+                sil[k] = pool.tile([P, PACK, width], F32, name="sil", bufs=2)
+            nc.scalar.activation(
+                out=sil[k][:, slots[0] : slots[-1] + 1, :],
+                in_=z_ps[k, i][:].rearrange("p (b n) -> p b n", b=len(slots)),
+                func=ACT.Silu,
+            )
+
+        def stt(k, i):
+            j, lo, width = ITEMS[k]
+            if i == 0:
+                h_raw[k] = pool.tile([P, PACK, width], BF16, name="h_raw", bufs=2, align_bytes=64)
+            for b, t in enumerate(slots_of(k, i)):
+                nc.vector.scalar_tensor_tensor(
+                    out=h_raw[k][:, t, :],
+                    in0=sil[k][:, t, :],
+                    scalar=c32[:, j, t : t + 1],
+                    in1=rc_ps[k, i][:, b * width : (b + 1) * width],
+                    op0=ALU.mult,
+                    op1=ALU.add,
+                )
+
+        def inter_h(k, lo, hi, engine=None):
+            engine = engine or ("s" if k in S_INTER_H else "v")
+            if k not in h_grp:
+                h_grp[k] = pool.tile([P, ITEMS[k][2], PACK], BF16, name="h_grp", bufs=2, align_bytes=64)
+            interleave(engine, h_grp[k][:, lo:hi, :], h_raw[k][:, :, lo:hi])
+
+        def quant_h(k, lo, hi):
+            j, first, width = ITEMS[k]
+            cols = slice(first + lo, first + hi)
+            quantize(h_codes[:, j, cols], h_scales[:, j, cols], h_grp[k][:, lo:hi, :].rearrange("p n t -> p (n t)"))
+
+        def stage2(dt, vh, heads, tag):
+            if 0 in heads:
+                acc[dt, vh] = psum.tile([P, W], F32, name="acc", tag=tag, bufs={"z": 3, "rc": 2, "acc": 3}[tag])
+            rows = slice(dt * P, (dt + 1) * P)
+            cols = slice(vh * W, (vh + 1) * W)
+            for j in heads:
+                nc.tensor.matmul_mx(
+                    out=acc[dt, vh][:],
+                    lhsT=h_codes[:, j, rows].bitcast(FP8X4),
+                    lhsT_scale=h_scales[:, j, rows],
+                    rhs=g_codes[:, j, cols].bitcast(FP8X4),
+                    rhs_scale=g_scales[:, j, cols],
+                    start=(j == 0),
+                    stop=(j == HEADS - 1),
+                )
+
+        def emit(dt, vh):
+            t = pool.tile([P, W], F32, name="result", bufs=6)
+            if (dt, vh) in V_EMIT:
+                nc.vector.tensor_copy(out=t[:], in_=acc[dt, vh][:])
+            else:
+                nc.scalar.copy(out=t[:], in_=acc[dt, vh][:])
+            nc.sync.dma_start(out=out[dt * P : (dt + 1) * P, vh * W : (vh + 1) * W], in_=t[:])
+
+        nc.scalar.dma_start(out=ws[:], in_=w_scale.rearrange("(g p t) o -> p g (t o)", p=P, t=PACK))
+        nc.scalar.dma_start(out=c16[:], in_=c.rearrange("j (p t) -> p j t", t=PACK))
+        load_w(0)
+        nc.sync.dma_start(out=x_raw[:], in_=x.rearrange("(p t) k -> p t k", t=PACK))
+        load_w(1)
+        nc.sync.dma_start(out=r_sb[:], in_=r.rearrange("(p t) k -> p t k", t=PACK))
+        load_g(0)
+        load_w(2)
+        load_g(1)
+        load_w(3)
+        load_g(2)
+
+        nc.vector.memset(warm[:], 0.0)
+        nc.scalar.activation(out=warm[:], in_=warm[:], func=ACT.Silu)
+        make_identity(nc, ident[:])
+        make_identity(nc, ident16[:])
+        nc.vector.tensor_copy(out=c32[:], in_=c16[:])
+        for i in range(HEADS * PACK):
+            nc.vector.tensor_scalar(out=diag[:, i, :], in0=ident16[:], scalar1=c32[:, i // PACK, i % PACK : i % PACK + 1], scalar2=None, op0=ALU.mult)
+
+        for i in range(8):
+            widen(0, i)
+        banks = {}
+        for gg in range(PASSES):
+            for pair in range(2):
+                banks[gg, pair] = x_transpose(gg, pair, "z" if gg == 0 else "acc")
+        inter_w(0, 0)
+        x_copy(0, 0, banks[0, 0], "s")
+        x_copy(0, 1, banks[0, 1], "s")
+        inter_w(0, 1)
+        x_copy(1, 0, banks[1, 0], "s")
+        x_copy(1, 1, banks[1, 1], "s")
+        quant_w(0, 0)
+        quant_x(0)
+        quant_w(0, 1)
+        quant_x(1)
+        for i in range(8):
+            widen(1, i)
+
+        groups = [(dt, vh) for dt in range(8) for vh in range(2)]
+        plan = {4: groups[0:2], 5: groups[2:4], 6: groups[4:6], 7: groups[6:8], 9: groups[8:10], 10: groups[10:12]}
+        pending = []
+        n_items = len(ITEMS)
+        last = n_items - 1
+
+        for k in range(n_items):
+            w1 = k + 1 if k + 1 < UNITS else None
+            w2 = k + 2 if k + 2 < UNITS else None
+            n = chunks(k)
+            if k == 0:
+                load_w(4)
+                load_g(3)
+                load_w(5)
+                load_w(6)
+                load_w(7)
+            for i in range(n):
+                zmm(k, i)
+                silu(k, i)
+                if w2 is not None:
+                    for q in range(8 * i // n, 8 * (i + 1) // n):
+                        widen(w2, q)
+            if w1 is not None:
+                inter_w(w1, 0)
+            else:
+                rcmm(k, 0)
+                stt(k, 0)
+            if k >= 1:
+                inter_h(k - 1, 0, ITEMS[k - 1][2])
+            if w1 is not None:
+                quant_w(w1, 0)
+                inter_w(w1, 1)
+            else:
+                rcmm(k, 1)
+                stt(k, 1)
+            if k >= 1:
+                quant_h(k - 1, 0, ITEMS[k - 1][2])
+            for key in pending:
+                quant_g(*key)
+            pending = []
+            if k < 4:
+                inter_g(k, 0)
+                inter_g(k, 1)
+                pending = [(k, 0), (k, 1)]
+            if w1 is not None:
+                quant_w(w1, 1)
+                for i in range(n):
+                    rcmm(k, i)
+                    stt(k, i)
+            for dt, vh in plan.get(k, []):
+                stage2(dt, vh, range(HEADS), "acc")
+                emit(dt, vh)
+
+        tags = {(6, 0): "acc", (6, 1): "acc", (7, 0): "acc", (7, 1): "z"}
+        for dt, vh in groups[12:]:
+            stage2(dt, vh, range(HEADS - 1), tags[dt, vh])
+        inter_h(last, 0, 128, "v")
+        inter_h(last, 128, 256, "s")
+        quant_h(last, 0, 128)
+        quant_h(last, 128, 256)
+        for dt, vh in groups[12:]:
+            stage2(dt, vh, [HEADS - 1], "")
+            emit(dt, vh)

@@ -14,7 +14,6 @@ E4M3 = mybir.dt.float8_e4m3fn
 FP8X4 = mybir.dt.float8_e4m3fn_x4
 ACT = mybir.ActivationFunctionType
 ALU = mybir.AluOpType
-ENG = mybir.EngineType
 
 P = 128
 PACK = 4
@@ -22,18 +21,36 @@ PASSES = D // 512
 W = 512
 UNITS = 8
 
-V_WIDEN = {0: 4, 1: 2, 4: 1}
-S_INTER_W = set()
-S_INTER_G = {(1, 0), (1, 1), (2, 0), (2, 1), (3, 0)}
-S_INTER_H = {5, 10}
-V_EMIT = {(4, 1), (7, 0)}
-ITEMS = [(j, 0, 512) for j in range(HEADS)] + [(j, lo, 256) for lo in (512, 768) for j in range(HEADS)]
+Q = 256
+ITEMS = [(j, lo) for lo in range(0, D, Q) for j in range(HEADS)]
+GROUPS = [(dt, vh) for dt in range(D // P) for vh in range(2)]
+
+V_WIDEN = {0: 2, 1: 4, 3: 1, 4: 1, 6: 2, 7: 1}
+S_INTER_W = {(2, 1)}
+S_INTER_G = {(0, 0), (2, 0), (3, 0), (3, 1)}
+G_ITEMS = range(1, 14)
+G_COLS = 192
+V_EMIT = {12, 14}
+G_PLAN = {0: [(0, 0)], 1: [(0, 1), (1, 0)], 2: [(1, 1)], 3: [(2, 0), (2, 1)], 4: [(3, 0)], 5: [(3, 1)]}
+EVERY = range(HEADS)
+PLAN = {
+    6: [(0, EVERY)],
+    7: [(1, EVERY), (2, EVERY)],
+    8: [(3, EVERY), (4, range(3))],
+    9: [(4, [3]), (5, EVERY)],
+    10: [(6, EVERY)],
+    11: [(7, EVERY)],
+    12: [(8, range(3)), (9, range(3))],
+    13: [(8, [3]), (9, [3]), (10, EVERY)],
+    14: [(11, EVERY)],
+    15: [(12, range(2)), (13, range(2)), (14, range(2)), (15, range(2))],
+}
 
 
 def tile_medusa_unembedding_grad_s7_kernel(tc, x, r, w_bytes, w_scale, c, g, out):
     nc = tc.nc
     with ExitStack() as ctx:
-        ctx.enter_context(tc.manual_schedule(engines={ENG.DVE, ENG.Activation, ENG.Pool, ENG.SP}))
+        ctx.enter_context(tc.manual_schedule())
         keep = ctx.enter_context(tc.tile_pool(name="keep", bufs=1))
         pool = ctx.enter_context(tc.tile_pool(name="pool", bufs=2))
         psum = ctx.enter_context(tc.psum_pool(name="psum", bufs=3))
@@ -55,7 +72,7 @@ def tile_medusa_unembedding_grad_s7_kernel(tc, x, r, w_bytes, w_scale, c, g, out
         h_codes = keep.tile([P, HEADS, D], U32, name="h_codes", align_bytes=64)
         h_scales = keep.tile([P, HEADS, D], U8, name="h_scales", align_bytes=64)
 
-        w_view = w_bytes.rearrange("(g p t) (j h n) -> g j h p t n", p=P, t=PACK, j=HEADS, h=2)
+        w_view = w_bytes.rearrange("(g p t) n -> g p t n", p=P, t=PACK)
         g_view = g.rearrange("(j p t) v -> j p t v", p=P, t=PACK)
 
         w8 = {}
@@ -75,7 +92,10 @@ def tile_medusa_unembedding_grad_s7_kernel(tc, x, r, w_bytes, w_scale, c, g, out
         def load_w(u):
             for gg in range(PASSES):
                 t = pool.tile([P, PACK, W], U8, name="w8", bufs=16)
-                nc.sync.dma_start(out=t[:], in_=w_view[gg, u % 4, u // 4])
+                at = 0
+                for j, lo in ITEMS[2 * u : 2 * u + 2]:
+                    nc.sync.dma_start(out=t[:, :, at : at + Q], in_=w_view[gg, :, :, D * j + lo : D * j + lo + Q])
+                    at += Q
                 w8[u, gg] = t
 
         def load_g(j):
@@ -99,8 +119,10 @@ def tile_medusa_unembedding_grad_s7_kernel(tc, x, r, w_bytes, w_scale, c, g, out
             s4 = src.rearrange("p t (c i) -> p c t i", i=4)
             if engine == "v":
                 nc.vector.tensor_copy(out=d4, in_=s4)
-            else:
+            elif engine == "s":
                 nc.scalar.copy(out=d4, in_=s4)
+            else:
+                nc.gpsimd.tensor_scalar(out=dst, in0=src.rearrange("p t n -> p n t"), scalar1=1.0, scalar2=0.0, op0=ALU.mult, op1=ALU.add)
 
         def inter_w(u, gg):
             engine = "s" if (u, gg) in S_INTER_W else "v"
@@ -112,8 +134,8 @@ def tile_medusa_unembedding_grad_s7_kernel(tc, x, r, w_bytes, w_scale, c, g, out
             nc.vector.quantize_mx(out=codes.bitcast(FP8X4), scales=scales, in_=src)
 
         def quant_w(u, gg):
-            tc_ = pool.tile([P, W], U32, name="w_codes", bufs=10, align_bytes=64)
-            ts_ = pool.tile([P, W], U8, name="w_scales", bufs=10, align_bytes=64)
+            tc_ = pool.tile([P, W], U32, name="w_codes", bufs=6, align_bytes=64)
+            ts_ = pool.tile([P, W], U8, name="w_scales", bufs=6, align_bytes=64)
             quantize(tc_[:], ts_[:], w_grp[u, gg][:].rearrange("p n t -> p (n t)"))
             w_codes[u, gg] = tc_
             w_scales[u, gg] = ts_
@@ -149,89 +171,70 @@ def tile_medusa_unembedding_grad_s7_kernel(tc, x, r, w_bytes, w_scale, c, g, out
         def quant_x(gg):
             quantize(x_codes[:, gg, :], x_scales[:, gg, :], x_grp[:, gg].rearrange("p b m k -> p (b m k)"))
 
-        def slots_of(k, i):
-            width = ITEMS[k][2]
-            per = W // width
-            return [i * per + b for b in range(per)]
-
-        def chunks(k):
-            return ITEMS[k][2] * PACK // W
-
         def zmm(k, i):
-            j, lo, width = ITEMS[k]
-            u, off = (lo // W) * 4 + j, lo % W
-            z = psum.tile([P, W], F32, name="z_ps", tag="z", bufs=3)
-            for b, t in enumerate(slots_of(k, i)):
-                rows = slice(t * P, (t + 1) * P)
+            u, off = k // 2, Q * (k % 2)
+            z = psum.tile([P, 2, Q], F32, name="z_ps", tag="z", bufs=3)
+            for b in range(2):
+                rows = slice((2 * i + b) * P, (2 * i + b + 1) * P)
                 for gg in range(PASSES):
                     nc.tensor.matmul_mx(
-                        out=z[:, b * width : (b + 1) * width],
+                        out=z[:, b, :],
                         lhsT=x_codes[:, gg, rows].bitcast(FP8X4),
                         lhsT_scale=x_scales[:, gg, rows],
-                        rhs=w_codes[u, gg][:, off : off + width].bitcast(FP8X4),
-                        rhs_scale=w_scales[u, gg][:, off : off + width],
+                        rhs=w_codes[u, gg][:, off : off + Q].bitcast(FP8X4),
+                        rhs_scale=w_scales[u, gg][:, off : off + Q],
                         start=(gg == 0),
                         stop=(gg == PASSES - 1),
                     )
             z_ps[k, i] = z
 
         def rcmm(k, i):
-            j, lo, width = ITEMS[k]
-            rc = psum.tile([P, W], F32, name="rc_ps", tag="rc", bufs=2)
-            for b, t in enumerate(slots_of(k, i)):
-                nc.tensor.matmul(
-                    out=rc[:, b * width : (b + 1) * width],
-                    lhsT=diag[:, j * PACK + t, :],
-                    rhs=r_sb[:, t, lo : lo + width],
-                    start=True,
-                    stop=True,
-                )
+            j, lo = ITEMS[k]
+            rc = psum.tile([P, 2, Q], F32, name="rc_ps", tag="rc", bufs=2)
+            for b in range(2):
+                t = 2 * i + b
+                nc.tensor.matmul(out=rc[:, b, :], lhsT=diag[:, j * PACK + t, :], rhs=r_sb[:, t, lo : lo + Q], start=True, stop=True)
             rc_ps[k, i] = rc
 
         def silu(k, i):
-            j, lo, width = ITEMS[k]
-            slots = slots_of(k, i)
             if i == 0:
-                sil[k] = pool.tile([P, PACK, width], F32, name="sil", bufs=2)
-            nc.scalar.activation(
-                out=sil[k][:, slots[0] : slots[-1] + 1, :],
-                in_=z_ps[k, i][:].rearrange("p (b n) -> p b n", b=len(slots)),
-                func=ACT.Silu,
-            )
+                sil[k] = pool.tile([P, PACK, Q], F32, name="sil", bufs=3)
+            nc.scalar.activation(out=sil[k][:, 2 * i : 2 * i + 2, :], in_=z_ps[k, i][:], func=ACT.Silu)
 
         def stt(k, i):
-            j, lo, width = ITEMS[k]
+            j, lo = ITEMS[k]
             if i == 0:
-                h_raw[k] = pool.tile([P, PACK, width], BF16, name="h_raw", bufs=2, align_bytes=64)
-            for b, t in enumerate(slots_of(k, i)):
+                h_raw[k] = pool.tile([P, PACK, Q], BF16, name="h_raw", bufs=3, align_bytes=64)
+            for b in range(2):
+                t = 2 * i + b
                 nc.vector.scalar_tensor_tensor(
                     out=h_raw[k][:, t, :],
                     in0=sil[k][:, t, :],
                     scalar=c32[:, j, t : t + 1],
-                    in1=rc_ps[k, i][:, b * width : (b + 1) * width],
+                    in1=rc_ps[k, i][:, b, :],
                     op0=ALU.mult,
                     op1=ALU.add,
                 )
 
-        def inter_h(k, lo, hi, engine=None):
-            engine = engine or ("s" if k in S_INTER_H else "v")
+        def inter_h(k, lo, hi, engine):
             if k not in h_grp:
-                h_grp[k] = pool.tile([P, ITEMS[k][2], PACK], BF16, name="h_grp", bufs=2, align_bytes=64)
+                h_grp[k] = pool.tile([P, Q, PACK], BF16, name="h_grp", bufs=1, align_bytes=64)
             interleave(engine, h_grp[k][:, lo:hi, :], h_raw[k][:, :, lo:hi])
 
         def quant_h(k, lo, hi):
-            j, first, width = ITEMS[k]
+            j, first = ITEMS[k]
             cols = slice(first + lo, first + hi)
             quantize(h_codes[:, j, cols], h_scales[:, j, cols], h_grp[k][:, lo:hi, :].rearrange("p n t -> p (n t)"))
 
-        def stage2(dt, vh, heads, tag):
+        def stage2(i, heads, tag):
+            dt, vh = GROUPS[i]
             if 0 in heads:
-                acc[dt, vh] = psum.tile([P, W], F32, name="acc", tag=tag, bufs={"z": 3, "rc": 2, "acc": 3}[tag])
+                acc[i] = psum.tile([P, W], F32, name="acc", tag=tag, bufs=3)
             rows = slice(dt * P, (dt + 1) * P)
             cols = slice(vh * W, (vh + 1) * W)
             for j in heads:
                 nc.tensor.matmul_mx(
-                    out=acc[dt, vh][:],
+                    out=acc[i][:],
                     lhsT=h_codes[:, j, rows].bitcast(FP8X4),
                     lhsT_scale=h_scales[:, j, rows],
                     rhs=g_codes[:, j, cols].bitcast(FP8X4),
@@ -240,12 +243,13 @@ def tile_medusa_unembedding_grad_s7_kernel(tc, x, r, w_bytes, w_scale, c, g, out
                     stop=(j == HEADS - 1),
                 )
 
-        def emit(dt, vh):
+        def emit(i):
+            dt, vh = GROUPS[i]
             t = pool.tile([P, W], F32, name="result", bufs=6)
-            if (dt, vh) in V_EMIT:
-                nc.vector.tensor_copy(out=t[:], in_=acc[dt, vh][:])
+            if i in V_EMIT:
+                nc.vector.tensor_copy(out=t[:], in_=acc[i][:])
             else:
-                nc.scalar.copy(out=t[:], in_=acc[dt, vh][:])
+                nc.scalar.copy(out=t[:], in_=acc[i][:])
             nc.sync.dma_start(out=out[dt * P : (dt + 1) * P, vh * W : (vh + 1) * W], in_=t[:])
 
         nc.scalar.dma_start(out=ws[:], in_=w_scale.rearrange("(g p t) o -> p g (t o)", p=P, t=PACK))
@@ -284,69 +288,73 @@ def tile_medusa_unembedding_grad_s7_kernel(tc, x, r, w_bytes, w_scale, c, g, out
         quant_x(0)
         quant_w(0, 1)
         quant_x(1)
-        for i in range(8):
+        for i in range(4):
             widen(1, i)
 
-        groups = [(dt, vh) for dt in range(8) for vh in range(2)]
-        plan = {4: groups[0:2], 5: groups[2:4], 6: groups[4:6], 7: groups[6:8], 9: groups[8:10], 10: groups[10:12]}
-        pending = []
         n_items = len(ITEMS)
         last = n_items - 1
-
+        zmm(0, 0)
+        zmm(0, 1)
+        rcmm(0, 0)
+        rcmm(0, 1)
+        pending = []
+        load_w(4)
+        load_g(3)
+        load_w(5)
+        load_w(6)
+        load_w(7)
         for k in range(n_items):
-            w1 = k + 1 if k + 1 < UNITS else None
-            w2 = k + 2 if k + 2 < UNITS else None
-            n = chunks(k)
-            if k == 0:
-                load_w(4)
-                load_g(3)
-                load_w(5)
-                load_w(6)
-                load_w(7)
-            for i in range(n):
-                zmm(k, i)
+            more = k < last
+            pieces = [] if k + 2 >= n_items else [(1 + k // 2, k % 2)]
+            wide_next = [(p, t) for p in ([((k + 3) // 2, (k + 3) % 2)] if k + 3 < n_items else []) for t in range(PACK)]
+            for i in range(2):
                 silu(k, i)
-                if w2 is not None:
-                    for q in range(8 * i // n, 8 * (i + 1) // n):
-                        widen(w2, q)
-            if w1 is not None:
-                inter_w(w1, 0)
-            else:
-                rcmm(k, 0)
-                stt(k, 0)
-            if k >= 1:
-                inter_h(k - 1, 0, ITEMS[k - 1][2])
-            if w1 is not None:
-                quant_w(w1, 0)
-                inter_w(w1, 1)
-            else:
-                rcmm(k, 1)
-                stt(k, 1)
-            if k >= 1:
-                quant_h(k - 1, 0, ITEMS[k - 1][2])
+                for (u, gg), t in wide_next[2 * i : 2 * i + 2]:
+                    widen(u, 4 * gg + t)
+            for i, heads in PLAN.get(k - 1, []):
+                if HEADS - 1 in heads:
+                    emit(i)
+            for piece in pieces:
+                inter_w(*piece)
+            if k >= 2:
+                inter_h(k - 2, G_COLS if k - 2 in G_ITEMS else 0, Q, "v")
             for key in pending:
                 quant_g(*key)
-            pending = []
-            if k < 4:
-                inter_g(k, 0)
-                inter_g(k, 1)
-                pending = [(k, 0), (k, 1)]
-            if w1 is not None:
-                quant_w(w1, 1)
-                for i in range(n):
-                    rcmm(k, i)
-                    stt(k, i)
-            for dt, vh in plan.get(k, []):
-                stage2(dt, vh, range(HEADS), "acc")
-                emit(dt, vh)
+            pending = G_PLAN.get(k, [])
+            if pending:
+                inter_g(*pending[0])
+            for piece in pieces:
+                quant_w(*piece)
+            for key in pending[1:]:
+                inter_g(*key)
+            if k >= 2:
+                quant_h(k - 2, 0, Q)
+            if k - 1 in G_ITEMS:
+                inter_h(k - 1, 0, G_COLS, "g")
+            if k == last:
+                inter_h(k - 1, 0, Q, "s")
+            stt(k, 0)
+            stt(k, 1)
+            todo = [(i, [j]) for i, heads in PLAN.get(k, []) for j in heads]
+            half = len(todo) // 2
+            if more:
+                zmm(k + 1, 0)
+                zmm(k + 1, 1)
+                rcmm(k + 1, 0)
+            for i, heads in todo[:half]:
+                stage2(i, heads, "z" if i == 15 else "acc")
+            if more:
+                rcmm(k + 1, 1)
+            for i, heads in todo[half:]:
+                stage2(i, heads, "z" if i == 15 else "acc")
 
-        tags = {(6, 0): "acc", (6, 1): "acc", (7, 0): "acc", (7, 1): "z"}
-        for dt, vh in groups[12:]:
-            stage2(dt, vh, range(HEADS - 1), tags[dt, vh])
-        inter_h(last, 0, 128, "v")
-        inter_h(last, 128, 256, "s")
-        quant_h(last, 0, 128)
-        quant_h(last, 128, 256)
-        for dt, vh in groups[12:]:
-            stage2(dt, vh, [HEADS - 1], "")
-            emit(dt, vh)
+        quant_h(last - 1, 0, Q)
+        for i in range(12, 16):
+            stage2(i, [2], "")
+        inter_h(last, 0, Q // 2, "v")
+        inter_h(last, Q // 2, Q, "s")
+        quant_h(last, 0, Q // 2)
+        quant_h(last, Q // 2, Q)
+        for i in range(12, 16):
+            stage2(i, [HEADS - 1], "")
+            emit(i)

@@ -25,25 +25,31 @@ Q = 256
 ITEMS = [(j, lo) for lo in range(0, D, Q) for j in range(HEADS)]
 GROUPS = [(dt, vh) for dt in range(D // P) for vh in range(2)]
 
-V_WIDEN = {0: 2, 1: 4, 3: 1, 4: 1, 6: 2, 7: 1}
-S_INTER_W = {(2, 1)}
-S_INTER_G = {(0, 0), (2, 0), (3, 0), (3, 1)}
-G_ITEMS = range(1, 14)
+V_WIDEN = {0: 3, 1: 3, 2: 3, 3: 1, 5: 1, 7: 1}
+S_INTER_W = set()
+PAIRED = set()
+S_INTER_G = {(0, 1), (1, 0), (1, 1), (2, 1), (3, 0)}
+LEAD = 3
+G_ITEMS = range(1, 13)
+S_INTER_H = {13}
 G_COLS = 192
-V_EMIT = {12, 14}
-G_PLAN = {0: [(0, 0)], 1: [(0, 1), (1, 0)], 2: [(1, 1)], 3: [(2, 0), (2, 1)], 4: [(3, 0)], 5: [(3, 1)]}
+V_EMIT = {8, 10, 15}
+G_PLAN = {1: [(0, 0), (0, 1), (1, 0)], 3: [(1, 1), (2, 0), (2, 1)], 4: [(3, 0), (3, 1)]}
 EVERY = range(HEADS)
 PLAN = {
-    6: [(0, EVERY)],
-    7: [(1, EVERY), (2, EVERY)],
-    8: [(3, EVERY), (4, range(3))],
-    9: [(4, [3]), (5, EVERY)],
-    10: [(6, EVERY)],
-    11: [(7, EVERY)],
-    12: [(8, range(3)), (9, range(3))],
-    13: [(8, [3]), (9, [3]), (10, EVERY)],
-    14: [(11, EVERY)],
-    15: [(12, range(2)), (13, range(2)), (14, range(2)), (15, range(2))],
+    2: [(0, [0])],
+    3: [(1, [0])],
+    5: [(0, [1, 2, 3]), (1, [1, 2, 3]), (2, [0, 1, 2])],
+    6: [(2, [3]), (3, [0, 1])],
+    7: [(3, [2, 3]), (4, [0])],
+    8: [(4, [1]), (5, [0, 1]), (6, [0, 1, 2])],
+    9: [(4, [2, 3]), (5, [2, 3])],
+    10: [(6, [3]), (7, EVERY), (8, [0])],
+    11: [(8, [1]), (9, [0, 1]), (10, [0, 1])],
+    12: [(8, [2]), (9, [2])],
+    13: [(8, [3]), (9, [3]), (10, [2])],
+    14: [(10, [3]), (11, EVERY), (12, [0])],
+    15: [(12, [1]), (13, [0, 1]), (14, [0, 1]), (15, [0, 1])],
 }
 
 
@@ -105,11 +111,13 @@ def tile_medusa_unembedding_grad_s7_kernel(tc, x, r, w_bytes, w_scale, c, g, out
 
         def widen(u, i):
             gg, t = i // PACK, i % PACK
+            paired = (u, gg) in PAIRED
             if t == 0:
-                wide[u, gg] = pool.tile([P, PACK, W], BF16, name="wide", bufs=4, align_bytes=64)
+                shape = [P, 2, W, 2] if paired else [P, PACK, W]
+                wide[u, gg] = pool.tile(shape, BF16, name="wide", bufs=4, align_bytes=64)
             src = w8[u, gg][:, t, :].bitcast(E4M3)
-            dst = wide[u, gg][:, t, :]
-            if i % 2 == 1 and i // 2 < V_WIDEN.get(u, 0):
+            dst = wide[u, gg][:, t // 2, :, t % 2] if paired else wide[u, gg][:, t, :]
+            if paired or i % 2 == 1 and i // 2 < V_WIDEN.get(u, 0):
                 nc.vector.tensor_scalar(out=dst, in0=src, scalar1=ws[:, gg, t : t + 1], scalar2=None, op0=ALU.mult)
             else:
                 nc.scalar.activation(out=dst, in_=src, func=ACT.Copy, scale=ws[:, gg, t : t + 1])
@@ -127,7 +135,12 @@ def tile_medusa_unembedding_grad_s7_kernel(tc, x, r, w_bytes, w_scale, c, g, out
         def inter_w(u, gg):
             engine = "s" if (u, gg) in S_INTER_W else "v"
             t = pool.tile([P, W, PACK], BF16, name="w_grp", bufs=3, align_bytes=64)
-            interleave(engine, t[:], wide[u, gg][:])
+            if (u, gg) in PAIRED:
+                words = wide[u, gg][:].rearrange("p a n e -> p a (n e)").bitcast(F32)
+                dst = t[:].rearrange("p n t -> p (n t)").bitcast(F32).rearrange("p (n a) -> p n a", a=2)
+                nc.scalar.copy(out=dst, in_=words.rearrange("p a n -> p n a"))
+            else:
+                interleave(engine, t[:], wide[u, gg][:])
             w_grp[u, gg] = t
 
         def quantize(codes, scales, src):
@@ -218,7 +231,8 @@ def tile_medusa_unembedding_grad_s7_kernel(tc, x, r, w_bytes, w_scale, c, g, out
 
         def inter_h(k, lo, hi, engine):
             if k not in h_grp:
-                h_grp[k] = pool.tile([P, Q, PACK], BF16, name="h_grp", bufs=1, align_bytes=64)
+                late = k > G_ITEMS[-1]
+                h_grp[k] = pool.tile([P, Q, PACK], BF16, name="h_late" if late else "h_grp", bufs=2 if late else 1, align_bytes=64)
             interleave(engine, h_grp[k][:, lo:hi, :], h_raw[k][:, :, lo:hi])
 
         def quant_h(k, lo, hi):
@@ -255,11 +269,11 @@ def tile_medusa_unembedding_grad_s7_kernel(tc, x, r, w_bytes, w_scale, c, g, out
         nc.scalar.dma_start(out=ws[:], in_=w_scale.rearrange("(g p t) o -> p g (t o)", p=P, t=PACK))
         nc.scalar.dma_start(out=c16[:], in_=c.rearrange("j (p t) -> p j t", t=PACK))
         load_w(0)
-        nc.sync.dma_start(out=x_raw[:], in_=x.rearrange("(p t) k -> p t k", t=PACK))
         load_w(1)
+        nc.sync.dma_start(out=x_raw[:], in_=x.rearrange("(p t) k -> p t k", t=PACK))
+        load_w(2)
         nc.sync.dma_start(out=r_sb[:], in_=r.rearrange("(p t) k -> p t k", t=PACK))
         load_g(0)
-        load_w(2)
         load_g(1)
         load_w(3)
         load_g(2)
@@ -279,17 +293,21 @@ def tile_medusa_unembedding_grad_s7_kernel(tc, x, r, w_bytes, w_scale, c, g, out
             for pair in range(2):
                 banks[gg, pair] = x_transpose(gg, pair, "z" if gg == 0 else "acc")
         inter_w(0, 0)
-        x_copy(0, 0, banks[0, 0], "s")
-        x_copy(0, 1, banks[0, 1], "s")
-        inter_w(0, 1)
-        x_copy(1, 0, banks[1, 0], "s")
-        x_copy(1, 1, banks[1, 1], "s")
-        quant_w(0, 0)
-        quant_x(0)
-        quant_w(0, 1)
-        quant_x(1)
         for i in range(4):
             widen(1, i)
+        inter_w(0, 1)
+        quant_w(0, 0)
+        inter_w(1, 0)
+        quant_w(0, 1)
+        for i in range(4, 8):
+            widen(1, i)
+        x_copy(0, 0, banks[0, 0], "s")
+        x_copy(0, 1, banks[0, 1], "s")
+        quant_w(1, 0)
+        quant_x(0)
+        x_copy(1, 0, banks[1, 0], "s")
+        x_copy(1, 1, banks[1, 1], "s")
+        quant_x(1)
 
         n_items = len(ITEMS)
         last = n_items - 1
@@ -299,42 +317,47 @@ def tile_medusa_unembedding_grad_s7_kernel(tc, x, r, w_bytes, w_scale, c, g, out
         rcmm(0, 1)
         pending = []
         load_w(4)
-        load_g(3)
-        load_w(5)
-        load_w(6)
-        load_w(7)
         for k in range(n_items):
+            if k == 2:
+                load_g(3)
+                load_w(5)
+                load_w(6)
+                load_w(7)
             more = k < last
-            pieces = [] if k + 2 >= n_items else [(1 + k // 2, k % 2)]
-            wide_next = [(p, t) for p in ([((k + 3) // 2, (k + 3) % 2)] if k + 3 < n_items else []) for t in range(PACK)]
+            pieces = [divmod(k + LEAD, 2)] if k + LEAD < n_items else []
+            wide_next = [(p, t) for p in ([divmod(k + LEAD + 1, 2)] if k + LEAD + 1 < n_items else []) for t in range(PACK)]
             for i in range(2):
                 silu(k, i)
                 for (u, gg), t in wide_next[2 * i : 2 * i + 2]:
                     widen(u, 4 * gg + t)
-            for i, heads in PLAN.get(k - 1, []):
-                if HEADS - 1 in heads:
-                    emit(i)
             for piece in pieces:
-                inter_w(*piece)
-            if k >= 2:
+                if piece in PAIRED:
+                    inter_w(*piece)
+            if k >= 2 and k - 2 <= G_ITEMS[-1]:
                 inter_h(k - 2, G_COLS if k - 2 in G_ITEMS else 0, Q, "v")
+            for piece in pieces:
+                if piece not in PAIRED:
+                    inter_w(*piece)
             for key in pending:
                 quant_g(*key)
             pending = G_PLAN.get(k, [])
-            if pending:
-                inter_g(*pending[0])
-            for piece in pieces:
-                quant_w(*piece)
-            for key in pending[1:]:
+            for key in pending:
                 inter_g(*key)
-            if k >= 2:
+            for i, heads in PLAN.get(k - 1, []):
+                if HEADS - 1 in heads:
+                    emit(i)
+            if k >= 2 and k - 2 <= G_ITEMS[-1]:
                 quant_h(k - 2, 0, Q)
             if k - 1 in G_ITEMS:
                 inter_h(k - 1, 0, G_COLS, "g")
-            if k == last:
-                inter_h(k - 1, 0, Q, "s")
+            for piece in pieces:
+                quant_w(*piece)
             stt(k, 0)
+            if k - 1 > G_ITEMS[-1]:
+                inter_h(k - 1, 0, Q, "s" if k - 1 in S_INTER_H else "v")
             stt(k, 1)
+            if k - 1 > G_ITEMS[-1]:
+                quant_h(k - 1, 0, Q)
             todo = [(i, [j]) for i, heads in PLAN.get(k, []) for j in heads]
             half = len(todo) // 2
             if more:
@@ -348,7 +371,6 @@ def tile_medusa_unembedding_grad_s7_kernel(tc, x, r, w_bytes, w_scale, c, g, out
             for i, heads in todo[half:]:
                 stage2(i, heads, "z" if i == 15 else "acc")
 
-        quant_h(last - 1, 0, Q)
         for i in range(12, 16):
             stage2(i, [2], "")
         inter_h(last, 0, Q // 2, "v")

@@ -25,31 +25,31 @@ Q = 256
 ITEMS = [(j, lo) for lo in range(0, D, Q) for j in range(HEADS)]
 GROUPS = [(dt, vh) for dt in range(D // P) for vh in range(2)]
 
-V_WIDEN = {0: 3, 1: 3, 2: 3, 3: 1, 5: 1, 7: 1}
-S_INTER_W = set()
-PAIRED = set()
+V_WIDEN = {0: 3, 1: 4, 2: 3, 3: 1, 6: 1}
+S_INTER_W = {(0, 0), (0, 1), (2, 1)}
+PAIRED = {(0, 1), (2, 1)}
 S_INTER_G = {(0, 1), (1, 0), (1, 1), (2, 1), (3, 0)}
 LEAD = 3
 G_ITEMS = range(1, 13)
-S_INTER_H = {13}
+S_INTER_H = {14}
 G_COLS = 192
-V_EMIT = {8, 10, 15}
-G_PLAN = {1: [(0, 0), (0, 1), (1, 0)], 3: [(1, 1), (2, 0), (2, 1)], 4: [(3, 0), (3, 1)]}
+V_EMIT = {13, 15}
+G_PLAN = {1: [(0, 0), (0, 1)], 2: [(1, 0)], 3: [(1, 1), (2, 0), (2, 1)], 4: [(3, 0), (3, 1)]}
 EVERY = range(HEADS)
 PLAN = {
-    2: [(0, [0])],
-    3: [(1, [0])],
-    5: [(0, [1, 2, 3]), (1, [1, 2, 3]), (2, [0, 1, 2])],
-    6: [(2, [3]), (3, [0, 1])],
-    7: [(3, [2, 3]), (4, [0])],
-    8: [(4, [1]), (5, [0, 1]), (6, [0, 1, 2])],
-    9: [(4, [2, 3]), (5, [2, 3])],
-    10: [(6, [3]), (7, EVERY), (8, [0])],
-    11: [(8, [1]), (9, [0, 1]), (10, [0, 1])],
-    12: [(8, [2]), (9, [2])],
-    13: [(8, [3]), (9, [3]), (10, [2])],
-    14: [(10, [3]), (11, EVERY), (12, [0])],
-    15: [(12, [1]), (13, [0, 1]), (14, [0, 1]), (15, [0, 1])],
+    3: [(0, [0]), (1, [0])],
+    4: [(0, [1, 2]), (1, [1, 2]), (2, [0]), (3, [0, 1, 2])],
+    5: [(0, [3]), (1, [3]), (3, [3])],
+    6: [(2, [1]), (4, [0])],
+    7: [(2, [2, 3])],
+    8: [(5, [0]), (6, [0, 1]), (7, [0])],
+    9: [(4, [1, 2, 3]), (6, [2]), (7, [1, 2])],
+    10: [(5, [1, 2, 3]), (6, [3]), (7, [3])],
+    11: [(8, [0, 1]), (9, [0, 1]), (10, [0, 1]), (11, [0])],
+    12: [(9, [2]), (11, [1])],
+    13: [(8, [2, 3]), (9, [3]), (10, [2, 3]), (11, [2, 3])],
+    14: [(12, [0]), (13, [0]), (14, [0]), (15, [0])],
+    15: [(12, [1]), (13, [1]), (14, [1]), (15, [1])],
 }
 
 
@@ -164,7 +164,7 @@ def tile_medusa_unembedding_grad_s7_kernel(tc, x, r, w_bytes, w_scale, c, g, out
             quantize(g_codes[:, j, cols], g_scales[:, j, cols], g_grp[j, half][:].rearrange("p n t -> p (n t)"))
 
         def x_transpose(gg, pair, tag):
-            bank = psum.tile([P, 2, 2, P], F32, name="x_ps", tag=tag, bufs=3)
+            bank = psum.tile([P, 2, 2, P], F32, name="x_ps", tag=tag, bufs=4)
             words = x_raw[:].bitcast(F32)
             for b in range(2):
                 for e in range(2):
@@ -186,7 +186,7 @@ def tile_medusa_unembedding_grad_s7_kernel(tc, x, r, w_bytes, w_scale, c, g, out
 
         def zmm(k, i):
             u, off = k // 2, Q * (k % 2)
-            z = psum.tile([P, 2, Q], F32, name="z_ps", tag="z", bufs=3)
+            z = psum.tile([P, 2, Q], F32, name="z_ps", tag="z", bufs=2)
             for b in range(2):
                 rows = slice((2 * i + b) * P, (2 * i + b + 1) * P)
                 for gg in range(PASSES):
@@ -243,7 +243,7 @@ def tile_medusa_unembedding_grad_s7_kernel(tc, x, r, w_bytes, w_scale, c, g, out
         def stage2(i, heads, tag):
             dt, vh = GROUPS[i]
             if 0 in heads:
-                acc[i] = psum.tile([P, W], F32, name="acc", tag=tag, bufs=3)
+                acc[i] = psum.tile([P, W], F32, name="acc", tag=tag, bufs=4)
             rows = slice(dt * P, (dt + 1) * P)
             cols = slice(vh * W, (vh + 1) * W)
             for j in heads:
@@ -291,7 +291,7 @@ def tile_medusa_unembedding_grad_s7_kernel(tc, x, r, w_bytes, w_scale, c, g, out
         banks = {}
         for gg in range(PASSES):
             for pair in range(2):
-                banks[gg, pair] = x_transpose(gg, pair, "z" if gg == 0 else "acc")
+                banks[gg, pair] = x_transpose(gg, pair, "acc")
         inter_w(0, 0)
         for i in range(4):
             widen(1, i)
@@ -330,9 +330,6 @@ def tile_medusa_unembedding_grad_s7_kernel(tc, x, r, w_bytes, w_scale, c, g, out
                 silu(k, i)
                 for (u, gg), t in wide_next[2 * i : 2 * i + 2]:
                     widen(u, 4 * gg + t)
-            for piece in pieces:
-                if piece in PAIRED:
-                    inter_w(*piece)
             if k >= 2 and k - 2 <= G_ITEMS[-1]:
                 inter_h(k - 2, G_COLS if k - 2 in G_ITEMS else 0, Q, "v")
             for piece in pieces:
@@ -346,6 +343,9 @@ def tile_medusa_unembedding_grad_s7_kernel(tc, x, r, w_bytes, w_scale, c, g, out
             for i, heads in PLAN.get(k - 1, []):
                 if HEADS - 1 in heads:
                     emit(i)
+            for piece, t in wide_next[:1]:
+                if piece in PAIRED:
+                    inter_w(*piece)
             if k >= 2 and k - 2 <= G_ITEMS[-1]:
                 quant_h(k - 2, 0, Q)
             if k - 1 in G_ITEMS:
@@ -365,11 +365,11 @@ def tile_medusa_unembedding_grad_s7_kernel(tc, x, r, w_bytes, w_scale, c, g, out
                 zmm(k + 1, 1)
                 rcmm(k + 1, 0)
             for i, heads in todo[:half]:
-                stage2(i, heads, "z" if i == 15 else "acc")
+                stage2(i, heads, "acc")
             if more:
                 rcmm(k + 1, 1)
             for i, heads in todo[half:]:
-                stage2(i, heads, "z" if i == 15 else "acc")
+                stage2(i, heads, "acc")
 
         for i in range(12, 16):
             stage2(i, [2], "")

@@ -17,39 +17,37 @@ ALU = mybir.AluOpType
 
 P = 128
 PACK = 4
-PASSES = D // 512
-W = 512
-UNITS = 8
-
+PASSES = D // (P * PACK)
 Q = 256
-ITEMS = [(j, lo) for lo in range(0, D, Q) for j in range(HEADS)]
-GROUPS = [(dt, vh) for dt in range(D // P) for vh in range(2)]
+W = 512
 
-V_WIDEN = {0: 3, 1: 4, 2: 3, 3: 1, 6: 1}
-S_INTER_W = {(0, 0), (0, 1), (2, 1)}
-PAIRED = {(0, 1), (2, 1)}
-S_INTER_G = {(0, 1), (1, 0), (1, 1), (2, 1), (3, 0)}
+ITEMS = [(j, lo) for lo in range(0, D, Q) for j in range(HEADS)]
+LAST = len(ITEMS) - 1
+GROUPS = [(dt, vh) for dt in range(D // P) for vh in range(V // W)]
+
 LEAD = 3
 G_ITEMS = range(1, 13)
-S_INTER_H = {14}
 G_COLS = 192
-V_EMIT = {13, 15}
-G_PLAN = {1: [(0, 0), (0, 1)], 2: [(1, 0)], 3: [(1, 1), (2, 0), (2, 1)], 4: [(3, 0), (3, 1)]}
-EVERY = range(HEADS)
+
+V_WIDEN = {0: 2, 1: 3, 2: 3, 3: 2, 4: 2, 6: 2, 7: 2}
+S_INTER_G = {(0, 1), (1, 0), (2, 0), (2, 1), (3, 0)}
+S_INTER_H = {14}
+V_EMIT = {8, 9, 13, 15}
+G_PLAN = {1: [(0, 0), (0, 1), (1, 0)], 2: [(1, 1)], 3: [(2, 0)], 4: [(2, 1), (3, 0), (3, 1)]}
 PLAN = {
     3: [(0, [0]), (1, [0])],
-    4: [(0, [1, 2]), (1, [1, 2]), (2, [0]), (3, [0, 1, 2])],
-    5: [(0, [3]), (1, [3]), (3, [3])],
-    6: [(2, [1]), (4, [0])],
-    7: [(2, [2, 3])],
-    8: [(5, [0]), (6, [0, 1]), (7, [0])],
-    9: [(4, [1, 2, 3]), (6, [2]), (7, [1, 2])],
-    10: [(5, [1, 2, 3]), (6, [3]), (7, [3])],
-    11: [(8, [0, 1]), (9, [0, 1]), (10, [0, 1]), (11, [0])],
-    12: [(9, [2]), (11, [1])],
-    13: [(8, [2, 3]), (9, [3]), (10, [2, 3]), (11, [2, 3])],
-    14: [(12, [0]), (13, [0]), (14, [0]), (15, [0])],
-    15: [(12, [1]), (13, [1]), (14, [1]), (15, [1])],
+    4: [(1, [1]), (2, [0]), (3, [0, 1])],
+    5: [(0, [1, 2, 3]), (2, [1])],
+    6: [(1, [2, 3]), (3, [2, 3]), (4, [0])],
+    7: [(2, [2, 3]), (4, [1]), (5, [0])],
+    8: [(5, [1]), (6, [0, 1])],
+    9: [(4, [2, 3]), (5, [2, 3]), (7, [0, 1, 2])],
+    10: [(6, [2, 3]), (7, [3]), (8, [0])],
+    11: [(8, [1]), (9, [0, 1]), (10, [0, 1]), (11, [0])],
+    12: [(8, [2]), (10, [2])],
+    13: [(8, [3]), (9, [2, 3]), (10, [3]), (11, [1, 2, 3])],
+    14: [(12, [0]), (13, [0, 1]), (14, [0]), (15, [0])],
+    15: [(12, [1]), (14, [1]), (15, [1])],
 }
 
 
@@ -59,12 +57,12 @@ def tile_medusa_unembedding_grad_s7_kernel(tc, x, r, w_bytes, w_scale, c, g, out
         ctx.enter_context(tc.manual_schedule())
         keep = ctx.enter_context(tc.tile_pool(name="keep", bufs=1))
         pool = ctx.enter_context(tc.tile_pool(name="pool", bufs=2))
-        psum = ctx.enter_context(tc.psum_pool(name="psum", bufs=3))
+        psum = ctx.enter_context(tc.psum_pool(name="psum", bufs=2))
 
-        ws = keep.tile([P, PASSES, PACK], F32, name="ws")
+        scale_sb = keep.tile([P, PASSES, PACK], F32, name="scale_sb")
         c16 = keep.tile([P, HEADS, PACK], BF16, name="c16")
         c32 = keep.tile([P, HEADS, PACK], F32, name="c32")
-        ident = keep.tile([P, P], F32, name="ident")
+        ident32 = keep.tile([P, P], F32, name="ident32")
         ident16 = keep.tile([P, P], BF16, name="ident16")
         diag = keep.tile([P, HEADS * PACK, P], BF16, name="diag")
         warm = keep.tile([P, 1], F32, name="warm")
@@ -78,195 +76,179 @@ def tile_medusa_unembedding_grad_s7_kernel(tc, x, r, w_bytes, w_scale, c, g, out
         h_codes = keep.tile([P, HEADS, D], U32, name="h_codes", align_bytes=64)
         h_scales = keep.tile([P, HEADS, D], U8, name="h_scales", align_bytes=64)
 
-        w_view = w_bytes.rearrange("(g p t) n -> g p t n", p=P, t=PACK)
+        w_view = w_bytes.rearrange("(i p t) n -> i p t n", p=P, t=PACK)
         g_view = g.rearrange("(j p t) v -> j p t v", p=P, t=PACK)
 
-        w8 = {}
-        wide = {}
-        w_grp = {}
-        w_codes = {}
-        w_scales = {}
-        g_raw = {}
-        g_grp = {}
-        sil = {}
-        h_raw = {}
-        h_grp = {}
-        z_ps = {}
-        rc_ps = {}
-        acc = {}
+        w8, wide, w_grp, w_codes, w_scales = {}, {}, {}, {}, {}
+        g_raw, g_grp = {}, {}
+        silu_z, h_raw, h_grp = {}, {}, {}
+        z_ps, rc_ps, acc = {}, {}, {}
 
         def load_w(u):
-            for gg in range(PASSES):
-                t = pool.tile([P, PACK, W], U8, name="w8", bufs=16)
-                at = 0
-                for j, lo in ITEMS[2 * u : 2 * u + 2]:
-                    nc.sync.dma_start(out=t[:, :, at : at + Q], in_=w_view[gg, :, :, D * j + lo : D * j + lo + Q])
-                    at += Q
-                w8[u, gg] = t
+            for i in range(PASSES):
+                w8_tile = pool.tile([P, PACK, W], U8, name="w8_tile", bufs=16)
+                for b, (j, lo) in enumerate(ITEMS[2 * u : 2 * u + 2]):
+                    cols = slice(D * j + lo, D * j + lo + Q)
+                    nc.sync.dma_start(out=w8_tile[:, :, b * Q : (b + 1) * Q], in_=w_view[i, :, :, cols])
+                w8[u, i] = w8_tile
 
         def load_g(j):
-            t = pool.tile([P, PACK, V], BF16, name="g_raw", bufs=3)
-            nc.sync.dma_start(out=t[:], in_=g_view[j])
-            g_raw[j] = t
+            g_tile = pool.tile([P, PACK, V], BF16, name="g_tile", bufs=3)
+            nc.sync.dma_start(out=g_tile[:], in_=g_view[j])
+            g_raw[j] = g_tile
 
-        def widen(u, i):
-            gg, t = i // PACK, i % PACK
-            paired = (u, gg) in PAIRED
+        def widen(u, i, t):
             if t == 0:
-                shape = [P, 2, W, 2] if paired else [P, PACK, W]
-                wide[u, gg] = pool.tile(shape, BF16, name="wide", bufs=4, align_bytes=64)
-            src = w8[u, gg][:, t, :].bitcast(E4M3)
-            dst = wide[u, gg][:, t // 2, :, t % 2] if paired else wide[u, gg][:, t, :]
-            if paired or i % 2 == 1 and i // 2 < V_WIDEN.get(u, 0):
-                nc.vector.tensor_scalar(out=dst, in0=src, scalar1=ws[:, gg, t : t + 1], scalar2=None, op0=ALU.mult)
+                wide[u, i] = pool.tile([P, PACK, W], BF16, name="wide", bufs=4, align_bytes=64)
+            src = w8[u, i][:, t, :].bitcast(E4M3)
+            dst = wide[u, i][:, t, :]
+            scale = scale_sb[:, i, t : t + 1]
+            plane = PACK * i + t
+            if plane % 2 == 1 and plane // 2 < V_WIDEN.get(u, 0):
+                nc.vector.tensor_scalar(out=dst, in0=src, scalar1=scale, scalar2=None, op0=ALU.mult)
             else:
-                nc.scalar.activation(out=dst, in_=src, func=ACT.Copy, scale=ws[:, gg, t : t + 1])
+                nc.scalar.activation(out=dst, in_=src, func=ACT.Copy, scale=scale)
 
         def interleave(engine, dst, src):
-            d4 = dst.rearrange("p (c i) t -> p c t i", i=4)
-            s4 = src.rearrange("p t (c i) -> p c t i", i=4)
-            if engine == "v":
-                nc.vector.tensor_copy(out=d4, in_=s4)
-            elif engine == "s":
-                nc.scalar.copy(out=d4, in_=s4)
+            if engine == "gpsimd":
+                in0 = src.rearrange("p t n -> p n t")
+                nc.gpsimd.tensor_scalar(out=dst, in0=in0, scalar1=1.0, scalar2=0.0, op0=ALU.mult, op1=ALU.add)
+                return
+            dst4 = dst.rearrange("p (n i) t -> p n t i", i=4)
+            src4 = src.rearrange("p t (n i) -> p n t i", i=4)
+            if engine == "vector":
+                nc.vector.tensor_copy(out=dst4, in_=src4)
             else:
-                nc.gpsimd.tensor_scalar(out=dst, in0=src.rearrange("p t n -> p n t"), scalar1=1.0, scalar2=0.0, op0=ALU.mult, op1=ALU.add)
-
-        def inter_w(u, gg):
-            engine = "s" if (u, gg) in S_INTER_W else "v"
-            t = pool.tile([P, W, PACK], BF16, name="w_grp", bufs=3, align_bytes=64)
-            if (u, gg) in PAIRED:
-                words = wide[u, gg][:].rearrange("p a n e -> p a (n e)").bitcast(F32)
-                dst = t[:].rearrange("p n t -> p (n t)").bitcast(F32).rearrange("p (n a) -> p n a", a=2)
-                nc.scalar.copy(out=dst, in_=words.rearrange("p a n -> p n a"))
-            else:
-                interleave(engine, t[:], wide[u, gg][:])
-            w_grp[u, gg] = t
+                nc.scalar.copy(out=dst4, in_=src4)
 
         def quantize(codes, scales, src):
-            nc.vector.quantize_mx(out=codes.bitcast(FP8X4), scales=scales, in_=src)
+            nc.vector.quantize_mx(out=codes.bitcast(FP8X4), scales=scales, in_=src.rearrange("p n t -> p (n t)"))
 
-        def quant_w(u, gg):
-            tc_ = pool.tile([P, W], U32, name="w_codes", bufs=6, align_bytes=64)
-            ts_ = pool.tile([P, W], U8, name="w_scales", bufs=6, align_bytes=64)
-            quantize(tc_[:], ts_[:], w_grp[u, gg][:].rearrange("p n t -> p (n t)"))
-            w_codes[u, gg] = tc_
-            w_scales[u, gg] = ts_
+        def interleave_w(u, i):
+            w_grp[u, i] = pool.tile([P, W, PACK], BF16, name="w_grp", bufs=3, align_bytes=64)
+            interleave("vector", w_grp[u, i][:], wide[u, i][:])
 
-        def inter_g(j, half):
-            engine = "s" if (j, half) in S_INTER_G else "v"
-            t = pool.tile([P, W, PACK], BF16, name="g_grp", bufs=3, align_bytes=64)
-            interleave(engine, t[:], g_raw[j][:, :, half * W : (half + 1) * W])
-            g_grp[j, half] = t
+        def quantize_w(u, i):
+            w_codes[u, i] = pool.tile([P, W], U32, name="w_codes", bufs=6, align_bytes=64)
+            w_scales[u, i] = pool.tile([P, W], U8, name="w_scales", bufs=6, align_bytes=64)
+            quantize(w_codes[u, i][:], w_scales[u, i][:], w_grp[u, i][:])
 
-        def quant_g(j, half):
+        def interleave_g(j, half):
+            g_grp[j, half] = pool.tile([P, W, PACK], BF16, name="g_grp", bufs=3, align_bytes=64)
+            engine = "scalar" if (j, half) in S_INTER_G else "vector"
+            interleave(engine, g_grp[j, half][:], g_raw[j][:, :, half * W : (half + 1) * W])
+
+        def quantize_g(j, half):
             cols = slice(half * W, (half + 1) * W)
-            quantize(g_codes[:, j, cols], g_scales[:, j, cols], g_grp[j, half][:].rearrange("p n t -> p (n t)"))
+            quantize(g_codes[:, j, cols], g_scales[:, j, cols], g_grp[j, half][:])
 
-        def x_transpose(gg, pair, tag):
-            bank = psum.tile([P, 2, 2, P], F32, name="x_ps", tag=tag, bufs=4)
+        def transpose_x(i, pair):
+            bank = psum.tile([P, 2, 2, P], F32, name="x_bank", tag="acc", bufs=4)
             words = x_raw[:].bitcast(F32)
+            first = P * PACK // 2 * i
             for b in range(2):
                 for e in range(2):
-                    lo = 256 * gg
-                    nc.tensor.transpose(bank[:, b, e, :], words[:, 2 * pair + b, lo + e : lo + 256 : 2], ident[:])
+                    columns = words[:, 2 * pair + b, first + e : first + 2 * P : 2]
+                    nc.tensor.transpose(bank[:, b, e, :], columns, ident32[:])
             return bank
 
-        def x_copy(gg, pair, bank, engine):
-            dst = x_grp[:, gg, 2 * pair : 2 * pair + 2].rearrange("p b m k -> p b (m k)").bitcast(F32)
-            dst = dst.rearrange("p b (m e) -> p b m e", e=2)
-            src = bank[:].rearrange("p b e m -> p b m e")
-            if engine == "v":
-                nc.vector.tensor_copy(out=dst, in_=src)
-            else:
-                nc.scalar.copy(out=dst, in_=src)
+        def copy_x(i, pair, bank):
+            dst = x_grp[:, i, 2 * pair : 2 * pair + 2].rearrange("p b m k -> p b (m k)").bitcast(F32)
+            nc.scalar.copy(
+                out=dst.rearrange("p b (m e) -> p b m e", e=2),
+                in_=bank[:].rearrange("p b e m -> p b m e"),
+            )
 
-        def quant_x(gg):
-            quantize(x_codes[:, gg, :], x_scales[:, gg, :], x_grp[:, gg].rearrange("p b m k -> p (b m k)"))
+        def quantize_x(i):
+            quantize(x_codes[:, i, :], x_scales[:, i, :], x_grp[:, i].rearrange("p b m k -> p (b m) k"))
 
-        def zmm(k, i):
-            u, off = k // 2, Q * (k % 2)
-            z = psum.tile([P, 2, Q], F32, name="z_ps", tag="z", bufs=2)
+        def multiply_z(k, pair):
+            u, first = k // 2, Q * (k % 2)
+            cols = slice(first, first + Q)
+            z = psum.tile([P, 2, Q], F32, name="z", tag="z", bufs=2)
             for b in range(2):
-                rows = slice((2 * i + b) * P, (2 * i + b + 1) * P)
-                for gg in range(PASSES):
+                slot = slice((2 * pair + b) * P, (2 * pair + b + 1) * P)
+                for i in range(PASSES):
                     nc.tensor.matmul_mx(
                         out=z[:, b, :],
-                        lhsT=x_codes[:, gg, rows].bitcast(FP8X4),
-                        lhsT_scale=x_scales[:, gg, rows],
-                        rhs=w_codes[u, gg][:, off : off + Q].bitcast(FP8X4),
-                        rhs_scale=w_scales[u, gg][:, off : off + Q],
-                        start=(gg == 0),
-                        stop=(gg == PASSES - 1),
+                        lhsT=x_codes[:, i, slot].bitcast(FP8X4),
+                        lhsT_scale=x_scales[:, i, slot],
+                        rhs=w_codes[u, i][:, cols].bitcast(FP8X4),
+                        rhs_scale=w_scales[u, i][:, cols],
+                        start=(i == 0),
+                        stop=(i == PASSES - 1),
                     )
-            z_ps[k, i] = z
+            z_ps[k, pair] = z
 
-        def rcmm(k, i):
+        def multiply_rc(k, pair):
             j, lo = ITEMS[k]
-            rc = psum.tile([P, 2, Q], F32, name="rc_ps", tag="rc", bufs=2)
+            rc = psum.tile([P, 2, Q], F32, name="rc", tag="rc", bufs=2)
             for b in range(2):
-                t = 2 * i + b
-                nc.tensor.matmul(out=rc[:, b, :], lhsT=diag[:, j * PACK + t, :], rhs=r_sb[:, t, lo : lo + Q], start=True, stop=True)
-            rc_ps[k, i] = rc
+                t = 2 * pair + b
+                nc.tensor.matmul(
+                    out=rc[:, b, :], lhsT=diag[:, j * PACK + t, :], rhs=r_sb[:, t, lo : lo + Q], start=True, stop=True
+                )
+            rc_ps[k, pair] = rc
 
-        def silu(k, i):
-            if i == 0:
-                sil[k] = pool.tile([P, PACK, Q], F32, name="sil", bufs=3)
-            nc.scalar.activation(out=sil[k][:, 2 * i : 2 * i + 2, :], in_=z_ps[k, i][:], func=ACT.Silu)
+        def apply_silu(k, pair):
+            if pair == 0:
+                silu_z[k] = pool.tile([P, PACK, Q], F32, name="silu_z", bufs=3)
+            nc.scalar.activation(out=silu_z[k][:, 2 * pair : 2 * pair + 2, :], in_=z_ps[k, pair][:], func=ACT.Silu)
 
-        def stt(k, i):
-            j, lo = ITEMS[k]
-            if i == 0:
+        def make_h(k, pair):
+            j = ITEMS[k][0]
+            if pair == 0:
                 h_raw[k] = pool.tile([P, PACK, Q], BF16, name="h_raw", bufs=3, align_bytes=64)
             for b in range(2):
-                t = 2 * i + b
+                t = 2 * pair + b
                 nc.vector.scalar_tensor_tensor(
                     out=h_raw[k][:, t, :],
-                    in0=sil[k][:, t, :],
+                    in0=silu_z[k][:, t, :],
                     scalar=c32[:, j, t : t + 1],
-                    in1=rc_ps[k, i][:, b, :],
+                    in1=rc_ps[k, pair][:, b, :],
                     op0=ALU.mult,
                     op1=ALU.add,
                 )
 
-        def inter_h(k, lo, hi, engine):
+        def interleave_h(k, lo, hi, engine):
             if k not in h_grp:
-                late = k > G_ITEMS[-1]
-                h_grp[k] = pool.tile([P, Q, PACK], BF16, name="h_late" if late else "h_grp", bufs=2 if late else 1, align_bytes=64)
+                if k <= G_ITEMS[-1]:
+                    h_grp[k] = pool.tile([P, Q, PACK], BF16, name="h_grp", bufs=1, align_bytes=64)
+                else:
+                    h_grp[k] = pool.tile([P, Q, PACK], BF16, name="h_late", bufs=2, align_bytes=64)
             interleave(engine, h_grp[k][:, lo:hi, :], h_raw[k][:, :, lo:hi])
 
-        def quant_h(k, lo, hi):
+        def quantize_h(k, lo, hi):
             j, first = ITEMS[k]
             cols = slice(first + lo, first + hi)
-            quantize(h_codes[:, j, cols], h_scales[:, j, cols], h_grp[k][:, lo:hi, :].rearrange("p n t -> p (n t)"))
+            quantize(h_codes[:, j, cols], h_scales[:, j, cols], h_grp[k][:, lo:hi, :])
 
-        def stage2(i, heads, tag):
+        def multiply_du(i, j):
             dt, vh = GROUPS[i]
-            if 0 in heads:
-                acc[i] = psum.tile([P, W], F32, name="acc", tag=tag, bufs=4)
+            if j == 0:
+                acc[i] = psum.tile([P, W], F32, name="du_bank", tag="acc", bufs=4)
             rows = slice(dt * P, (dt + 1) * P)
             cols = slice(vh * W, (vh + 1) * W)
-            for j in heads:
-                nc.tensor.matmul_mx(
-                    out=acc[i][:],
-                    lhsT=h_codes[:, j, rows].bitcast(FP8X4),
-                    lhsT_scale=h_scales[:, j, rows],
-                    rhs=g_codes[:, j, cols].bitcast(FP8X4),
-                    rhs_scale=g_scales[:, j, cols],
-                    start=(j == 0),
-                    stop=(j == HEADS - 1),
-                )
+            nc.tensor.matmul_mx(
+                out=acc[i][:],
+                lhsT=h_codes[:, j, rows].bitcast(FP8X4),
+                lhsT_scale=h_scales[:, j, rows],
+                rhs=g_codes[:, j, cols].bitcast(FP8X4),
+                rhs_scale=g_scales[:, j, cols],
+                start=(j == 0),
+                stop=(j == HEADS - 1),
+            )
 
-        def emit(i):
+        def store_du(i):
             dt, vh = GROUPS[i]
-            t = pool.tile([P, W], F32, name="result", bufs=6)
+            result = pool.tile([P, W], F32, name="result", bufs=6)
             if i in V_EMIT:
-                nc.vector.tensor_copy(out=t[:], in_=acc[i][:])
+                nc.vector.tensor_copy(out=result[:], in_=acc[i][:])
             else:
-                nc.scalar.copy(out=t[:], in_=acc[i][:])
-            nc.sync.dma_start(out=out[dt * P : (dt + 1) * P, vh * W : (vh + 1) * W], in_=t[:])
+                nc.scalar.copy(out=result[:], in_=acc[i][:])
+            nc.sync.dma_start(out=out[dt * P : (dt + 1) * P, vh * W : (vh + 1) * W], in_=result[:])
 
-        nc.scalar.dma_start(out=ws[:], in_=w_scale.rearrange("(g p t) o -> p g (t o)", p=P, t=PACK))
+        nc.scalar.dma_start(out=scale_sb[:], in_=w_scale.rearrange("(i p t) o -> p i (t o)", p=P, t=PACK))
         nc.scalar.dma_start(out=c16[:], in_=c.rearrange("j (p t) -> p j t", t=PACK))
         load_w(0)
         load_w(1)
@@ -280,103 +262,105 @@ def tile_medusa_unembedding_grad_s7_kernel(tc, x, r, w_bytes, w_scale, c, g, out
 
         nc.vector.memset(warm[:], 0.0)
         nc.scalar.activation(out=warm[:], in_=warm[:], func=ACT.Silu)
-        make_identity(nc, ident[:])
+        make_identity(nc, ident32[:])
         make_identity(nc, ident16[:])
         nc.vector.tensor_copy(out=c32[:], in_=c16[:])
-        for i in range(HEADS * PACK):
-            nc.vector.tensor_scalar(out=diag[:, i, :], in0=ident16[:], scalar1=c32[:, i // PACK, i % PACK : i % PACK + 1], scalar2=None, op0=ALU.mult)
+        for j in range(HEADS):
+            for t in range(PACK):
+                nc.vector.tensor_scalar(
+                    out=diag[:, j * PACK + t, :],
+                    in0=ident16[:],
+                    scalar1=c32[:, j, t : t + 1],
+                    scalar2=None,
+                    op0=ALU.mult,
+                )
 
-        for i in range(8):
-            widen(0, i)
-        banks = {}
-        for gg in range(PASSES):
-            for pair in range(2):
-                banks[gg, pair] = x_transpose(gg, pair, "acc")
-        inter_w(0, 0)
-        for i in range(4):
-            widen(1, i)
-        inter_w(0, 1)
-        quant_w(0, 0)
-        inter_w(1, 0)
-        quant_w(0, 1)
-        for i in range(4, 8):
-            widen(1, i)
-        x_copy(0, 0, banks[0, 0], "s")
-        x_copy(0, 1, banks[0, 1], "s")
-        quant_w(1, 0)
-        quant_x(0)
-        x_copy(1, 0, banks[1, 0], "s")
-        x_copy(1, 1, banks[1, 1], "s")
-        quant_x(1)
+        for i in range(PASSES):
+            for t in range(PACK):
+                widen(0, i, t)
+        banks = {(i, pair): transpose_x(i, pair) for i in range(PASSES) for pair in range(2)}
+        interleave_w(0, 0)
+        for t in range(PACK):
+            widen(1, 0, t)
+        interleave_w(0, 1)
+        quantize_w(0, 0)
+        interleave_w(1, 0)
+        quantize_w(0, 1)
+        for t in range(PACK):
+            widen(1, 1, t)
+        for pair in range(2):
+            copy_x(0, pair, banks[0, pair])
+        quantize_w(1, 0)
+        quantize_x(0)
+        for pair in range(2):
+            copy_x(1, pair, banks[1, pair])
+        quantize_x(1)
 
-        n_items = len(ITEMS)
-        last = n_items - 1
-        zmm(0, 0)
-        zmm(0, 1)
-        rcmm(0, 0)
-        rcmm(0, 1)
-        pending = []
+        for pair in range(2):
+            multiply_z(0, pair)
+        for pair in range(2):
+            multiply_rc(0, pair)
         load_w(4)
-        for k in range(n_items):
+
+        for k in range(LAST + 1):
             if k == 2:
                 load_g(3)
-                load_w(5)
-                load_w(6)
-                load_w(7)
-            more = k < last
-            pieces = [divmod(k + LEAD, 2)] if k + LEAD < n_items else []
-            wide_next = [(p, t) for p in ([divmod(k + LEAD + 1, 2)] if k + LEAD + 1 < n_items else []) for t in range(PACK)]
-            for i in range(2):
-                silu(k, i)
-                for (u, gg), t in wide_next[2 * i : 2 * i + 2]:
-                    widen(u, 4 * gg + t)
-            if k >= 2 and k - 2 <= G_ITEMS[-1]:
-                inter_h(k - 2, G_COLS if k - 2 in G_ITEMS else 0, Q, "v")
-            for piece in pieces:
-                if piece not in PAIRED:
-                    inter_w(*piece)
-            for key in pending:
-                quant_g(*key)
-            pending = G_PLAN.get(k, [])
-            for key in pending:
-                inter_g(*key)
+                for u in range(5, 8):
+                    load_w(u)
+            piece = divmod(k + LEAD, PASSES) if k + LEAD <= LAST else None
+            next_piece = divmod(k + LEAD + 1, PASSES) if k + LEAD + 1 <= LAST else None
+
+            for pair in range(2):
+                apply_silu(k, pair)
+                if next_piece:
+                    for t in (2 * pair, 2 * pair + 1):
+                        widen(*next_piece, t)
+
+            early = 2 <= k <= G_ITEMS[-1] + 2
+            if early:
+                interleave_h(k - 2, G_COLS if k - 2 in G_ITEMS else 0, Q, "vector")
+            if piece:
+                interleave_w(*piece)
+            for half in G_PLAN.get(k - 1, []):
+                quantize_g(*half)
+            for half in G_PLAN.get(k, []):
+                interleave_g(*half)
             for i, heads in PLAN.get(k - 1, []):
                 if HEADS - 1 in heads:
-                    emit(i)
-            for piece, t in wide_next[:1]:
-                if piece in PAIRED:
-                    inter_w(*piece)
-            if k >= 2 and k - 2 <= G_ITEMS[-1]:
-                quant_h(k - 2, 0, Q)
+                    store_du(i)
+            if early:
+                quantize_h(k - 2, 0, Q)
             if k - 1 in G_ITEMS:
-                inter_h(k - 1, 0, G_COLS, "g")
-            for piece in pieces:
-                quant_w(*piece)
-            stt(k, 0)
-            if k - 1 > G_ITEMS[-1]:
-                inter_h(k - 1, 0, Q, "s" if k - 1 in S_INTER_H else "v")
-            stt(k, 1)
-            if k - 1 > G_ITEMS[-1]:
-                quant_h(k - 1, 0, Q)
-            todo = [(i, [j]) for i, heads in PLAN.get(k, []) for j in heads]
-            half = len(todo) // 2
-            if more:
-                zmm(k + 1, 0)
-                zmm(k + 1, 1)
-                rcmm(k + 1, 0)
-            for i, heads in todo[:half]:
-                stage2(i, heads, "acc")
-            if more:
-                rcmm(k + 1, 1)
-            for i, heads in todo[half:]:
-                stage2(i, heads, "acc")
+                interleave_h(k - 1, 0, G_COLS, "gpsimd")
+            if piece:
+                quantize_w(*piece)
 
-        for i in range(12, 16):
-            stage2(i, [2], "")
-        inter_h(last, 0, Q // 2, "v")
-        inter_h(last, Q // 2, Q, "s")
-        quant_h(last, 0, Q // 2)
-        quant_h(last, Q // 2, Q)
-        for i in range(12, 16):
-            stage2(i, [HEADS - 1], "")
-            emit(i)
+            late = k - 1 > G_ITEMS[-1]
+            make_h(k, 0)
+            if late:
+                interleave_h(k - 1, 0, Q, "scalar" if k - 1 in S_INTER_H else "vector")
+            make_h(k, 1)
+            if late:
+                quantize_h(k - 1, 0, Q)
+
+            passes = [(i, j) for i, heads in PLAN.get(k, []) for j in heads]
+            cut = len(passes) // 2
+            if k < LAST:
+                for pair in range(2):
+                    multiply_z(k + 1, pair)
+            for pair, share in enumerate((passes[:cut], passes[cut:])):
+                if k < LAST:
+                    multiply_rc(k + 1, pair)
+                for i, j in share:
+                    multiply_du(i, j)
+
+        last_groups = range(len(GROUPS) - 4, len(GROUPS))
+        for i in last_groups:
+            multiply_du(i, 2)
+        interleave_h(LAST, 0, Q // 2, "vector")
+        interleave_h(LAST, Q // 2, Q, "scalar")
+        quantize_h(LAST, 0, Q // 2)
+        quantize_h(LAST, Q // 2, Q)
+        for i in last_groups:
+            multiply_du(i, 3)
+            store_du(i)

from contextlib import ExitStack

import concourse.mybir as mybir
from concourse.masks import make_identity

T, HEADS, D, V = 512, 4, 1024, 1024
FLOPS = 2 * T * D * HEADS * D + 2 * D * HEADS * T * V

F32 = mybir.dt.float32
BF16 = mybir.dt.bfloat16
U32 = mybir.dt.uint32
U8 = mybir.dt.uint8
E4M3 = mybir.dt.float8_e4m3fn
FP8X4 = mybir.dt.float8_e4m3fn_x4
ACT = mybir.ActivationFunctionType
ALU = mybir.AluOpType

P = 128
PACK = 4
PASSES = D // (P * PACK)
Q = 256
W = 512

ITEMS = [(j, lo) for lo in range(0, D, Q) for j in range(HEADS)]
LAST = len(ITEMS) - 1
GROUPS = [(dt, vh) for dt in range(D // P) for vh in range(V // W)]

LEAD = 3
G_ITEMS = range(1, 13)
G_COLS = 192

V_WIDEN = {0: 2, 1: 3, 2: 3, 3: 2, 4: 2, 6: 2, 7: 2}
S_INTER_G = {(0, 1), (1, 0), (2, 0), (2, 1), (3, 0)}
S_INTER_H = {14}
V_EMIT = {8, 9, 13, 15}
G_PLAN = {1: [(0, 0), (0, 1), (1, 0)], 2: [(1, 1)], 3: [(2, 0)], 4: [(2, 1), (3, 0), (3, 1)]}
PLAN = {
    3: [(0, [0]), (1, [0])],
    4: [(1, [1]), (2, [0]), (3, [0, 1])],
    5: [(0, [1, 2, 3]), (2, [1])],
    6: [(1, [2, 3]), (3, [2, 3]), (4, [0])],
    7: [(2, [2, 3]), (4, [1]), (5, [0])],
    8: [(5, [1]), (6, [0, 1])],
    9: [(4, [2, 3]), (5, [2, 3]), (7, [0, 1, 2])],
    10: [(6, [2, 3]), (7, [3]), (8, [0])],
    11: [(8, [1]), (9, [0, 1]), (10, [0, 1]), (11, [0])],
    12: [(8, [2]), (10, [2])],
    13: [(8, [3]), (9, [2, 3]), (10, [3]), (11, [1, 2, 3])],
    14: [(12, [0]), (13, [0, 1]), (14, [0]), (15, [0])],
    15: [(12, [1]), (14, [1]), (15, [1])],
}


def tile_medusa_unembedding_grad_s7_kernel(tc, x, r, w_bytes, w_scale, c, g, out):
    nc = tc.nc
    with ExitStack() as ctx:
        ctx.enter_context(tc.manual_schedule())
        keep = ctx.enter_context(tc.tile_pool(name="keep", bufs=1))
        pool = ctx.enter_context(tc.tile_pool(name="pool", bufs=2))
        psum = ctx.enter_context(tc.psum_pool(name="psum", bufs=2))

        scale_sb = keep.tile([P, PASSES, PACK], F32, name="scale_sb")
        c16 = keep.tile([P, HEADS, PACK], BF16, name="c16")
        c32 = keep.tile([P, HEADS, PACK], F32, name="c32")
        ident32 = keep.tile([P, P], F32, name="ident32")
        ident16 = keep.tile([P, P], BF16, name="ident16")
        diag = keep.tile([P, HEADS * PACK, P], BF16, name="diag")
        warm = keep.tile([P, 1], F32, name="warm")
        x_raw = keep.tile([P, PACK, D], BF16, name="x_raw", align_bytes=64)
        x_grp = keep.tile([P, PASSES, PACK, P, PACK], BF16, name="x_grp", align_bytes=64)
        x_codes = keep.tile([P, PASSES, T], U32, name="x_codes", align_bytes=64)
        x_scales = keep.tile([P, PASSES, T], U8, name="x_scales", align_bytes=64)
        r_sb = keep.tile([P, PACK, D], BF16, name="r_sb")
        g_codes = keep.tile([P, HEADS, V], U32, name="g_codes", align_bytes=64)
        g_scales = keep.tile([P, HEADS, V], U8, name="g_scales", align_bytes=64)
        h_codes = keep.tile([P, HEADS, D], U32, name="h_codes", align_bytes=64)
        h_scales = keep.tile([P, HEADS, D], U8, name="h_scales", align_bytes=64)

        w_view = w_bytes.rearrange("(i p t) n -> i p t n", p=P, t=PACK)
        g_view = g.rearrange("(j p t) v -> j p t v", p=P, t=PACK)

        w8, wide, w_grp, w_codes, w_scales = {}, {}, {}, {}, {}
        g_raw, g_grp = {}, {}
        silu_z, h_raw, h_grp = {}, {}, {}
        z_ps, rc_ps, acc = {}, {}, {}

        def load_w(u):
            for i in range(PASSES):
                w8_tile = pool.tile([P, PACK, W], U8, name="w8_tile", bufs=16)
                for b, (j, lo) in enumerate(ITEMS[2 * u : 2 * u + 2]):
                    cols = slice(D * j + lo, D * j + lo + Q)
                    nc.sync.dma_start(out=w8_tile[:, :, b * Q : (b + 1) * Q], in_=w_view[i, :, :, cols])
                w8[u, i] = w8_tile

        def load_g(j):
            g_tile = pool.tile([P, PACK, V], BF16, name="g_tile", bufs=3)
            nc.sync.dma_start(out=g_tile[:], in_=g_view[j])
            g_raw[j] = g_tile

        def widen(u, i, t):
            if t == 0:
                wide[u, i] = pool.tile([P, PACK, W], BF16, name="wide", bufs=4, align_bytes=64)
            src = w8[u, i][:, t, :].bitcast(E4M3)
            dst = wide[u, i][:, t, :]
            scale = scale_sb[:, i, t : t + 1]
            plane = PACK * i + t
            if plane % 2 == 1 and plane // 2 < V_WIDEN.get(u, 0):
                nc.vector.tensor_scalar(out=dst, in0=src, scalar1=scale, scalar2=None, op0=ALU.mult)
            else:
                nc.scalar.activation(out=dst, in_=src, func=ACT.Copy, scale=scale)

        def interleave(engine, dst, src):
            if engine == "gpsimd":
                in0 = src.rearrange("p t n -> p n t")
                nc.gpsimd.tensor_scalar(out=dst, in0=in0, scalar1=1.0, scalar2=0.0, op0=ALU.mult, op1=ALU.add)
                return
            dst4 = dst.rearrange("p (n i) t -> p n t i", i=4)
            src4 = src.rearrange("p t (n i) -> p n t i", i=4)
            if engine == "vector":
                nc.vector.tensor_copy(out=dst4, in_=src4)
            else:
                nc.scalar.copy(out=dst4, in_=src4)

        def quantize(codes, scales, src):
            nc.vector.quantize_mx(out=codes.bitcast(FP8X4), scales=scales, in_=src.rearrange("p n t -> p (n t)"))

        def interleave_w(u, i):
            w_grp[u, i] = pool.tile([P, W, PACK], BF16, name="w_grp", bufs=3, align_bytes=64)
            interleave("vector", w_grp[u, i][:], wide[u, i][:])

        def quantize_w(u, i):
            w_codes[u, i] = pool.tile([P, W], U32, name="w_codes", bufs=6, align_bytes=64)
            w_scales[u, i] = pool.tile([P, W], U8, name="w_scales", bufs=6, align_bytes=64)
            quantize(w_codes[u, i][:], w_scales[u, i][:], w_grp[u, i][:])

        def interleave_g(j, half):
            g_grp[j, half] = pool.tile([P, W, PACK], BF16, name="g_grp", bufs=3, align_bytes=64)
            engine = "scalar" if (j, half) in S_INTER_G else "vector"
            interleave(engine, g_grp[j, half][:], g_raw[j][:, :, half * W : (half + 1) * W])

        def quantize_g(j, half):
            cols = slice(half * W, (half + 1) * W)
            quantize(g_codes[:, j, cols], g_scales[:, j, cols], g_grp[j, half][:])

        def transpose_x(i, pair):
            bank = psum.tile([P, 2, 2, P], F32, name="x_bank", tag="acc", bufs=4)
            words = x_raw[:].bitcast(F32)
            first = P * PACK // 2 * i
            for b in range(2):
                for e in range(2):
                    columns = words[:, 2 * pair + b, first + e : first + 2 * P : 2]
                    nc.tensor.transpose(bank[:, b, e, :], columns, ident32[:])
            return bank

        def copy_x(i, pair, bank):
            dst = x_grp[:, i, 2 * pair : 2 * pair + 2].rearrange("p b m k -> p b (m k)").bitcast(F32)
            nc.scalar.copy(
                out=dst.rearrange("p b (m e) -> p b m e", e=2),
                in_=bank[:].rearrange("p b e m -> p b m e"),
            )

        def quantize_x(i):
            quantize(x_codes[:, i, :], x_scales[:, i, :], x_grp[:, i].rearrange("p b m k -> p (b m) k"))

        def multiply_z(k, pair):
            u, first = k // 2, Q * (k % 2)
            cols = slice(first, first + Q)
            z = psum.tile([P, 2, Q], F32, name="z", tag="z", bufs=2)
            for b in range(2):
                slot = slice((2 * pair + b) * P, (2 * pair + b + 1) * P)
                for i in range(PASSES):
                    nc.tensor.matmul_mx(
                        out=z[:, b, :],
                        lhsT=x_codes[:, i, slot].bitcast(FP8X4),
                        lhsT_scale=x_scales[:, i, slot],
                        rhs=w_codes[u, i][:, cols].bitcast(FP8X4),
                        rhs_scale=w_scales[u, i][:, cols],
                        start=(i == 0),
                        stop=(i == PASSES - 1),
                    )
            z_ps[k, pair] = z

        def multiply_rc(k, pair):
            j, lo = ITEMS[k]
            rc = psum.tile([P, 2, Q], F32, name="rc", tag="rc", bufs=2)
            for b in range(2):
                t = 2 * pair + b
                nc.tensor.matmul(
                    out=rc[:, b, :], lhsT=diag[:, j * PACK + t, :], rhs=r_sb[:, t, lo : lo + Q], start=True, stop=True
                )
            rc_ps[k, pair] = rc

        def apply_silu(k, pair):
            if pair == 0:
                silu_z[k] = pool.tile([P, PACK, Q], F32, name="silu_z", bufs=3)
            nc.scalar.activation(out=silu_z[k][:, 2 * pair : 2 * pair + 2, :], in_=z_ps[k, pair][:], func=ACT.Silu)

        def make_h(k, pair):
            j = ITEMS[k][0]
            if pair == 0:
                h_raw[k] = pool.tile([P, PACK, Q], BF16, name="h_raw", bufs=3, align_bytes=64)
            for b in range(2):
                t = 2 * pair + b
                nc.vector.scalar_tensor_tensor(
                    out=h_raw[k][:, t, :],
                    in0=silu_z[k][:, t, :],
                    scalar=c32[:, j, t : t + 1],
                    in1=rc_ps[k, pair][:, b, :],
                    op0=ALU.mult,
                    op1=ALU.add,
                )

        def interleave_h(k, lo, hi, engine):
            if k not in h_grp:
                if k <= G_ITEMS[-1]:
                    h_grp[k] = pool.tile([P, Q, PACK], BF16, name="h_grp", bufs=1, align_bytes=64)
                else:
                    h_grp[k] = pool.tile([P, Q, PACK], BF16, name="h_late", bufs=2, align_bytes=64)
            interleave(engine, h_grp[k][:, lo:hi, :], h_raw[k][:, :, lo:hi])

        def quantize_h(k, lo, hi):
            j, first = ITEMS[k]
            cols = slice(first + lo, first + hi)
            quantize(h_codes[:, j, cols], h_scales[:, j, cols], h_grp[k][:, lo:hi, :])

        def multiply_du(i, j):
            dt, vh = GROUPS[i]
            if j == 0:
                acc[i] = psum.tile([P, W], F32, name="du_bank", tag="acc", bufs=4)
            rows = slice(dt * P, (dt + 1) * P)
            cols = slice(vh * W, (vh + 1) * W)
            nc.tensor.matmul_mx(
                out=acc[i][:],
                lhsT=h_codes[:, j, rows].bitcast(FP8X4),
                lhsT_scale=h_scales[:, j, rows],
                rhs=g_codes[:, j, cols].bitcast(FP8X4),
                rhs_scale=g_scales[:, j, cols],
                start=(j == 0),
                stop=(j == HEADS - 1),
            )

        def store_du(i):
            dt, vh = GROUPS[i]
            result = pool.tile([P, W], F32, name="result", bufs=6)
            if i in V_EMIT:
                nc.vector.tensor_copy(out=result[:], in_=acc[i][:])
            else:
                nc.scalar.copy(out=result[:], in_=acc[i][:])
            nc.sync.dma_start(out=out[dt * P : (dt + 1) * P, vh * W : (vh + 1) * W], in_=result[:])

        nc.scalar.dma_start(out=scale_sb[:], in_=w_scale.rearrange("(i p t) o -> p i (t o)", p=P, t=PACK))
        nc.scalar.dma_start(out=c16[:], in_=c.rearrange("j (p t) -> p j t", t=PACK))
        load_w(0)
        load_w(1)
        nc.sync.dma_start(out=x_raw[:], in_=x.rearrange("(p t) k -> p t k", t=PACK))
        load_w(2)
        nc.sync.dma_start(out=r_sb[:], in_=r.rearrange("(p t) k -> p t k", t=PACK))
        load_g(0)
        load_g(1)
        load_w(3)
        load_g(2)

        nc.vector.memset(warm[:], 0.0)
        nc.scalar.activation(out=warm[:], in_=warm[:], func=ACT.Silu)
        make_identity(nc, ident32[:])
        make_identity(nc, ident16[:])
        nc.vector.tensor_copy(out=c32[:], in_=c16[:])
        for j in range(HEADS):
            for t in range(PACK):
                nc.vector.tensor_scalar(
                    out=diag[:, j * PACK + t, :],
                    in0=ident16[:],
                    scalar1=c32[:, j, t : t + 1],
                    scalar2=None,
                    op0=ALU.mult,
                )

        for i in range(PASSES):
            for t in range(PACK):
                widen(0, i, t)
        banks = {(i, pair): transpose_x(i, pair) for i in range(PASSES) for pair in range(2)}
        interleave_w(0, 0)
        for t in range(PACK):
            widen(1, 0, t)
        interleave_w(0, 1)
        quantize_w(0, 0)
        interleave_w(1, 0)
        quantize_w(0, 1)
        for t in range(PACK):
            widen(1, 1, t)
        for pair in range(2):
            copy_x(0, pair, banks[0, pair])
        quantize_w(1, 0)
        quantize_x(0)
        for pair in range(2):
            copy_x(1, pair, banks[1, pair])
        quantize_x(1)

        for pair in range(2):
            multiply_z(0, pair)
        for pair in range(2):
            multiply_rc(0, pair)
        load_w(4)

        for k in range(LAST + 1):
            if k == 2:
                load_g(3)
                for u in range(5, 8):
                    load_w(u)
            piece = divmod(k + LEAD, PASSES) if k + LEAD <= LAST else None
            next_piece = divmod(k + LEAD + 1, PASSES) if k + LEAD + 1 <= LAST else None

            for pair in range(2):
                apply_silu(k, pair)
                if next_piece:
                    for t in (2 * pair, 2 * pair + 1):
                        widen(*next_piece, t)

            early = 2 <= k <= G_ITEMS[-1] + 2
            if early:
                interleave_h(k - 2, G_COLS if k - 2 in G_ITEMS else 0, Q, "vector")
            if piece:
                interleave_w(*piece)
            for half in G_PLAN.get(k - 1, []):
                quantize_g(*half)
            for half in G_PLAN.get(k, []):
                interleave_g(*half)
            for i, heads in PLAN.get(k - 1, []):
                if HEADS - 1 in heads:
                    store_du(i)
            if early:
                quantize_h(k - 2, 0, Q)
            if k - 1 in G_ITEMS:
                interleave_h(k - 1, 0, G_COLS, "gpsimd")
            if piece:
                quantize_w(*piece)

            late = k - 1 > G_ITEMS[-1]
            make_h(k, 0)
            if late:
                interleave_h(k - 1, 0, Q, "scalar" if k - 1 in S_INTER_H else "vector")
            make_h(k, 1)
            if late:
                quantize_h(k - 1, 0, Q)

            passes = [(i, j) for i, heads in PLAN.get(k, []) for j in heads]
            cut = len(passes) // 2
            if k < LAST:
                for pair in range(2):
                    multiply_z(k + 1, pair)
            for pair, share in enumerate((passes[:cut], passes[cut:])):
                if k < LAST:
                    multiply_rc(k + 1, pair)
                for i, j in share:
                    multiply_du(i, j)

        last_groups = range(len(GROUPS) - 4, len(GROUPS))
        for i in last_groups:
            multiply_du(i, 2)
        interleave_h(LAST, 0, Q // 2, "vector")
        interleave_h(LAST, Q // 2, Q, "scalar")
        quantize_h(LAST, 0, Q // 2)
        quantize_h(LAST, Q // 2, Q)
        for i in last_groups:
            multiply_du(i, 3)
            store_du(i)
